import numpy as np, ml_dtypes
CORES = [40,64,80,88,96,104,120,144]
N = 8
import mx_ref
BF = ml_dtypes.bfloat16
def entries(a):
    return np.ascontiguousarray(a.T).reshape(-1)
def table(e):
    return np.ascontiguousarray(np.reshape(e, (-1, 16)).T).astype(np.int32)
def f(rng, *shape):
    return mx_ref.flush((rng.standard_normal(shape, dtype=np.float32) * np.exp2(rng.integers(-2, 3, shape[:-1] + (1,)))).astype(BF))
def wide(rng, *shape, cols=0):
    v = rng.standard_normal(shape, dtype=np.float32) * np.exp2(rng.integers(-12, 13, shape)).astype(np.float32)
    if cols: v *= np.repeat(np.exp2(rng.integers(-cols, cols + 1, shape[:-2] + (1, shape[-1] // 4))) * (rng.random(shape[:-2] + (1, shape[-1] // 4)) > 0.0625), 4, axis=-1).astype(np.float32)
    return mx_ref.flush(v.astype(BF))
T, ND, CD, LM, CAPP = 512, 64, 16, 64, 128
def lens(rng, n, total):
    a = 1 + np.minimum(LM - 1, rng.multinomial(total - n, rng.dirichlet(np.ones(n))))
    for i in rng.permutation(n): a[i] += min(LM - a[i], total - a.sum())
    return a
def places(rng, l):
    o = rng.permutation(ND); g = rng.multinomial(T - l.sum(), rng.dirichlet(np.ones(ND + 1)))
    s = np.zeros(ND, int); s[o] = np.cumsum(g[:ND]) + np.cumsum(l[o]) - l[o]
    return s
def pick(rng, l):
    p = rng.permutation(ND); a, b = p[:CD].copy(), p[CD:].copy()
    while l[a].sum() > CAPP:
        i = np.argmax(l[a]); j = rng.choice(np.flatnonzero(l[b] < l[a[i]]))
        a[i], b[j] = b[j], a[i]
    return rng.permutation(a)
def lists(rng, kind="any"):
    s, n, c = [], [], np.zeros((N, N * CD), int)
    K, J = (T - ND) // (LM - 1), (CAPP - CD) // (LM - 1)
    TT = min(T, ND // CD * CAPP)
    for q in range(N):
        d = rng.permutation(ND); l = np.ones(ND, int)
        if kind == "long": l[d[:K]] = LM
        elif kind == "full": l[d] = np.concatenate([lens(rng, CD, CAPP), lens(rng, CD, CAPP), lens(rng, ND - 2 * CD, T - 2 * CAPP)])
        elif kind == "any": l[d] = lens(rng, ND, int(rng.integers(TT - TT // 4, TT + 1)))
        s.append(table(places(rng, l))); n.append(table(l))
        for r in range(N):
            if kind == "long": e = rng.permutation(np.concatenate([rng.permutation(d[:K])[:J], rng.permutation(d[K:])[:CD - J]]))
            elif kind == "full": k = CD * int(rng.integers(0, 2)); e = rng.permutation(d[k:k + CD])
            else: e = pick(rng, l)
            c[r, CD * q:CD * q + CD] = e
    return {"st": np.stack(s), "ln": np.stack(n), "cd": np.stack([table(c[r]) for r in range(N)])}
def setup_inputs(rng):
    return {"x": f(rng, N, 128, 4 * T), "qw": f(rng, N, 128, 512), **lists(rng)}
def setup_inputs_long(rng):
    return {**setup_inputs(rng), **lists(rng, "long")}
def setup_inputs_ones(rng):
    return {**setup_inputs(rng), **lists(rng, "ones")}
def setup_inputs_full(rng):
    return {**setup_inputs(rng), **lists(rng, "full")}
def setup_inputs_below(rng):
    d = setup_inputs(rng); p = rng.permutation(N)
    s, u = rng.integers(-20, 27, N), rng.integers(-20, 28, N)
    s[p[0]] = 26; u[rng.choice(p[:-1])] = 27; s[p[-1]] = 0; u[p[-1]] = 0
    d["x"] = mx_ref.flush((-np.exp2(rng.uniform(-3, 3, (N, 128, 4 * T)) + s[:, None, None])).astype(BF))
    d["qw"] = mx_ref.flush(np.exp2(rng.uniform(-2, 2, (N, 128, 512)) + u[:, None, None]).astype(BF))
    return d
def setup_inputs_spread(rng):
    d = setup_inputs(rng); d["x"] = wide(rng, N, 128, 4 * T, cols=8); return d
def check_inputs(d):
    b = []
    L = [entries(d["ln"][r]).astype(np.int64) for r in range(N)]
    for r in range(N):
        s, l = entries(d["st"][r]).astype(np.int64), L[r]
        if l.min() < 1 or l.max() > LM: b.append("ln")
        o = np.argsort(s, kind="stable")
        if s.min() < 0 or (s + l).max() > T or (s[o][:-1] + l[o][:-1] > s[o][1:]).any(): b.append("st")
        c = entries(d["cd"][r])
        if c.min() < 0 or c.max() >= ND: b.append("cd"); continue
        for q in range(N):
            e = c[CD * q:CD * q + CD]
            if len(set(e.tolist())) != CD or L[q][e].sum() > CAPP: b.append("cd")
    return sorted(set(b))
def reference(x, qw, st, ln, cd):
    X = [mx_ref.quantize(x[q]) for q in range(N)]
    y = np.zeros((N, 128, N * CD), np.float32)
    for r in range(N):
        W = mx_ref.quantize(qw[r]); c = entries(cd[r])
        for q in range(N):
            z = mx_ref.matmul(W, X[q]); s, l = entries(st[q]), entries(ln[q])
            for i in range(CD * q, CD * q + CD):
                y[r][:, i] = z[:, s[c[i]]:s[c[i]] + l[c[i]]].max(axis=1)
    return {"y": y}

@@ -1,0 +1,391 @@
+from concourse.bass import DstId, RemoteDMATransfer
+from concourse.mybir import dt, AluOpType as A, ActivationFunctionType as F
+
+N, TOK, CAP = 8, 512, 128
+BIG, FAR, LIFT = 1.0e29, 1.0e6, 4096.0
+VB = {"S": 0, "O": 392, "M": 912}
+VW = {"S": 392, "O": 520, "M": 136}
+GB = {"S": 0, "O": 56, "M": 128}
+EB = {"S": 0, "O": 4, "M": 8}
+PB = {"S": 0, "O": 3, "M": 7}
+
+SCRATCH = {
+    "cdi": ("sbuf", [128, 8], "int32"), "cdu": ("sbuf", [128, 8], "uint16"), "cdm": ("sbuf", [128, 2], "uint16"),
+    "row": ("sbuf", [1, 128], "int32"), "tab": ("sbuf", [128, 128], "int32"),
+    "stt": ("sbuf", [128, 64], "float32"), "lnt": ("sbuf", [128, 64], "float32"),
+    "poi": ("sbuf", [128, 4], "int32"), "poa": ("sbuf", [128, 4], "int32"), "pou": ("sbuf", [128, 4], "uint16"),
+    "pp": ("sbuf", [128, 1], "int32"), "ki": ("sbuf", [128, 3], "int32"), "kf": ("sbuf", [128, 3], "float32"),
+    "cst": ("sbuf", [128, 1], "float32"),
+    "ii": ("sbuf", [128, 64], "float32"), "jj": ("sbuf", [128, 128], "float32"),
+    "le": ("sbuf", [128, 64], "float32"), "dmb": ("sbuf", [128, 128], "float32"), "dmk": ("sbuf", [128, 128], "float32"),
+    "rst": ("sbuf", [128, 64], "float32"), "far": ("sbuf", [128, 64], "float32"), "neg": ("sbuf", [128, 16], "float32"),
+    "cds": ("sbuf", [128, 4], "uint16"), "cdo": ("sbuf", [128, 4], "uint16"),
+    "g1": ("sbuf", [128, 152], "float32"), "s1": ("sbuf", [128, 152], "float32"), "g2": ("sbuf", [128, 152], "float32"),
+    "en0": ("sbuf", [128, 16], "uint16"),
+    "vv": ("sbuf", [128, 1096], "float32"), "d0": ("sbuf", [128, 1048], "float32"),
+    "la": ("sbuf", [128, 1024], "float32"), "lb": ("sbuf", [128, 1024], "float32"),
+    "off": ("sbuf", [128, 256], "uint16"),
+    "xs": ("sbuf", [128, 4 * (TOK + CAP)], "bfloat16"), "ws": ("sbuf", [128, 512], "bfloat16"),
+    "tile": ("sbuf", [128, 4096], "bfloat16"),
+    "qc": ("sbuf", [128, 1024], "float8_e4m3fn_x4"), "qp": ("sbuf", [128, 1024], "uint8"),
+    "wc": ("sbuf", [128, 128], "float8_e4m3fn_x4"), "wp": ("sbuf", [128, 128], "uint8"),
+    "lc": ("sbuf", [128, 896], "float8_e4m3fn_x4"), "lp": ("sbuf", [128, 896], "uint8"),
+    "el": ("sbuf", [128, 16], "uint16"), "ea": ("sbuf", [128, 8], "int32"), "eb": ("sbuf", [128, 8], "int32"),
+    "en": ("sbuf", [128, 16], "uint16"),
+    "mk": ("sbuf", [128, 1096], "float32"), "so": ("sbuf", [128, 1024], "float32"), "ys": ("sbuf", [128, 128], "float32"),
+    "ps": ("psum", [128, 4096], "float32"),
+    "hcd": ("sbuf", [128, 2], "uint16"), "hen": ("sbuf", [128, 2], "uint16"),
+    "hc": ("sbuf", [128, 128], "float8_e4m3fn_x4"), "hp": ("sbuf", [128, 128], "uint8"),
+}
+SEMAPHORES = (["vec", "act", "pe", "gc", "lcd", "ltab", "lx", "lw", "ly", "sent", "cds", "cdo", "ens", "eno",
+               "hcd", "hen", "hc", "hp"] + ["t%d" % s for s in range(7)])
+
+
+def groups(T, topo, r):
+    own = [q for q in range(N) if q == r or topo.may_write(T.cores[r], T.cores[q])]
+    oth = [q for q in range(N) if q not in own]
+    a = own.index(r)
+    return [own[(a + j) % len(own)] for j in range(len(own))], [oth[(a + k) % len(oth)] for k in range(len(oth))], a
+
+
+def helpers(T, topo, r):
+    c = T.cores[r]
+    dst = T.cores[groups(T, topo, r)[1][0]]
+    hs = [h for h in topo.cores_of(c) if h != c and topo.may_write(h, dst)]
+    near = [h for h in hs if topo.die(h) == topo.die(c)]
+    far = [h for h in hs if topo.die(h) != topo.die(c)]
+    return [near[0], far[0], far[1], near[1]]
+
+
+def part(e, i, n):
+    w = len(e) // n
+    return e[i * w:(i + 1) * w]
+
+
+def bits(e):
+    return sum(1 << x for x in e)
+
+
+def lane_up(topo, c, h, k):
+    e = topo.engines(c, h)
+    return part(e[len(e) // 2:], k, 4)
+
+
+def lane_same(topo, c, d, j):
+    return part(topo.engines(c, d), j - 1, 4)
+
+
+def u8(ap):
+    return ap.bitcast(dt.uint8)
+
+
+def hand_on(g, core, T, topo, r, k):
+    _, oth, a = groups(T, topo, r)
+    d = oth[k]
+    dc, rc = T.cores[d], T.cores[r]
+    slot = (a - groups(T, topo, d)[2]) % 4
+    rid, pid = topo.addr(dc, core)
+    e = topo.engines(core, dc)
+    n_up = len(lane_up(topo, rc, core, k))
+    sent = [0]
+
+    def on(dst, src, sem, eng):
+        g.remote_dma(dst, src, T.sem[sem], T.sem.sent, pid, rid, bits(eng))
+        sent[0] += len(eng)
+
+    g.wait_ge(T.sem.hcd, n_up)
+    on(T.cdo[:, slot:slot + 1], T.hcd[:, 0:1], "cdo", part(e, 0, 2))
+    g.wait_ge(T.sem.hen, n_up)
+    on(T.el[:, 6 + 2 * slot:7 + 2 * slot], T.hen[:, 0:1], "eno", part(e, 1, 2))
+    s = 3 + slot
+    g.wait_ge(T.sem.hc, len(topo.engines(rc, core)) // 2)
+    on(u8(T.lc[:, 128 * s:128 * s + 128]), u8(T.hc[:, 0:128]), "t%d" % s, e)
+    g.wait_ge(T.sem.hp, len(topo.engines(rc, core)) // 4)
+    on(T.lp[:, 128 * s:128 * s + 128], T.hp[:, 0:128], "t%d" % s, e)
+    g.wait_ge(T.sem.sent, sent[0])
+
+
+def rank_program(g, core, T, topo):
+    rank = T.rank_of(core)
+    if rank is None:
+        for r in range(N):
+            if T.cores[r] in topo.cores_of(core):
+                hs = helpers(T, topo, r)
+                if core in hs:
+                    hand_on(g, core, T, topo, r, hs.index(core))
+        return
+    own, oth, a = groups(T, topo, rank)
+    hs = helpers(T, topo, rank)
+    v, sc, pe = g.vector, g.scalar, g.tensor
+    queue = {"v": v, "s": sc, "t": pe, "g": g, "y": g.sync}
+    cnt = {"vec": 0, "act": 0, "pe": 0, "gc": 0, "sent": 0}
+    seen = {}
+
+    def need(q, sem, val):
+        if seen.get((q, sem), 0) < val:
+            queue[q].wait_ge(T.sem[sem], int(val))
+            seen[(q, sem)] = val
+
+    def done(sem, ins):
+        cnt[sem] += 1
+        ins.then_inc(T.sem[sem], 1)
+        return cnt[sem]
+
+    def V(ins):
+        return done("vec", ins)
+
+    def S(ins):
+        return done("act", ins)
+
+    for i in range(8):
+        (g.sync if i % 2 == 0 else sc).dma_start(T.cdi[16 * i:16 * i + 16, :], T.cd[:]).then_inc(T.sem.lcd, 16)
+    g.sync.dma_start(T.row[0:1, 0:64], T.st[:]).then_inc(T.sem.ltab, 16)
+    sc.dma_start(T.row[0:1, 64:128], T.ln[:]).then_inc(T.sem.ltab, 16)
+    g.sync.dma_start(T.xs[:, 0:4 * TOK], T.x[:]).then_inc(T.sem.lx, 16)
+    sc.dma_start(T.ws[:], T.qw[:]).then_inc(T.sem.lw, 16)
+
+    done("gc", g.iota(T.pp[:], [[0, 1]], 0, 1))
+    done("gc", g.iota(T.poi[:], [[1, 4]], 0, 4))
+    done("gc", g.iota(T.ii[:], [[0, 4], [1, 16]], 0, 0, allow_small_or_imprecise_dtypes=True))
+    done("gc", g.iota(T.jj[:], [[0, 32], [1, 4]], 0, 0, allow_small_or_imprecise_dtypes=True))
+
+    i_z = V(v.memset(T.vv[:], 0.0))
+    need("s", "vec", i_z)
+    i_d0 = S(sc.activation(T.d0[:], T.vv[:, 0:1048], F.Copy, bias=4.0))
+    i_mk = S(sc.activation(T.mk[:], T.vv[:], F.Copy, bias=BIG))
+
+    need("v", "lcd", 128)
+    i_cd = V(v.tensor_copy(T.cdu[:], T.cdi[:]))
+    need("g", "vec", i_cd)
+
+    def fused(trs):
+        ts = []
+        for dc, dst, src, sem, e in trs:
+            rid, pid = topo.addr(dc, core)
+            ts.append(RemoteDMATransfer(dst_ids=[DstId(rid=rid, pnc=pid)], dma_engine_mask=bits(e),
+                                        remote_sem=T.sem[sem], src=src, dst=dst))
+            cnt["sent"] += len(e)
+        g.remote_dma_fused(ts, local_sem=T.sem.sent)
+
+    def at(d):
+        return (a - groups(T, topo, d)[2]) % 4
+
+    fused([(hs[k], T.hcd[:, 0:1], T.cdu[:, oth[k]:oth[k] + 1], "hcd", lane_up(topo, core, hs[k], k)) for k in range(4)])
+    fused([(T.cores[own[j]], T.cds[:, at(own[j]) - 1:at(own[j])], T.cdu[:, own[j]:own[j] + 1], "cds",
+            lane_same(topo, core, T.cores[own[j]], j)) for j in range(1, 4)])
+    need("g", "ltab", 32)
+    i_tab = done("gc", g.partition_broadcast(T.tab[:], T.row[0:1, :], 128))
+
+    V(v.memset(T.g2[:], 0.0))
+    V(v.memset(T.far[:], -FAR))
+    V(v.memset(T.neg[:], -BIG))
+    V(v.memset(T.xs[:, 4 * TOK:], 0.0))
+    i_r = V(v.memset(T.rst[:], 0.0))
+    need("v", "gc", 4)
+    V(v.tensor_scalar(T.ki[:, 0:1], T.pp[:], 15, None, A.bitwise_and))
+    V(v.tensor_scalar(T.ki[:, 1:2], T.pp[:], 3, None, A.bitwise_and))
+    i_k = V(v.tensor_scalar(T.ki[:, 2:3], T.pp[:], 15, 2, A.bitwise_and, A.arith_shift_right))
+    i_p = V(v.tensor_scalar(T.poa[:], T.poi[:], 63, None, A.bitwise_and))
+    need("v", "vec", i_k)
+    i_k = V(v.tensor_copy(T.kf[:], T.ki[:]))
+    need("v", "vec", i_p)
+    i_p = V(v.tensor_copy(T.pou[:], T.poa[:]))
+    for b in range(1, 4):
+        V(v.memset(T.rst[:, 16 * b:16 * b + 1], 128.0 * b))
+    need("v", "vec", i_k)
+    V(v.tensor_scalar(T.le[:], T.ii[:], T.kf[:, 0:1], None, A.is_le))
+    i_m = V(v.tensor_scalar(T.dmb[:], T.jj[:], T.kf[:, 2:3], FAR + LIFT, A.is_gt, A.mult))
+    V(v.tensor_scalar(T.cst[:], T.kf[:, 2:3], -3.0, LIFT, A.add, A.mult))
+    need("v", "vec", i_m)
+    V(v.tensor_scalar(T.dmk[:], T.dmb[:], -FAR, None, A.add))
+    need("v", "act", i_d0)
+    V(v.memset(T.d0[:, 0:384:128], 0.0))
+    V(v.memset(T.d0[:, 392:904:128], 0.0))
+    V(v.memset(T.d0[:, 912:913], 0.0))
+    need("v", "gc", i_tab)
+    need("v", "vec", i_p)
+    V(v.tensor_copy(T.stt[:], T.tab[:, 0:64].indirect(T.pou[:, 0:4])))
+    i_ln = V(v.tensor_copy(T.lnt[:], T.tab[:, 64:128].indirect(T.pou[:, 0:4])))
+
+    def ends(bt, R, off, sem, val):
+        gb, eb, vb, vw = GB[bt], EB[bt], VB[bt], VW[bt]
+        w = 16 * R
+        if sem:
+            need("v", sem, val)
+            need("s", sem, val)
+        need("v", "vec", i_ln)
+        need("s", "vec", i_ln)
+        i_g2 = S(sc.activation(T.g2[:, gb:gb + w], T.stt[:, 0:64].indirect(off), F.Identity, bias=T.kf[:, 1:2], scale=4.0))
+        i = V(v.tensor_tensor(T.g1[:, gb:gb + w], T.lnt[:, 0:64].indirect(off), T.le[:, 0:w], A.mult))
+        need("v", "vec", i)
+        i = V(v.tensor_tensor_scan(T.s1[:, gb:gb + w], T.rst[:, 0:w], T.g1[:, gb:gb + w], 0.0, A.max, A.add))
+        need("v", "vec", i)
+        i_e = V(v.tensor_copy(T.en0[:, eb:eb + R], T.s1[:, gb + 15:gb + w:16]))
+        need("v", "vec", i_e)
+        V(v.tensor_copy(T.d0[:, vb:vb + vw].indirect(T.en0[:, eb:eb + R]), T.far[:, 0:w]))
+        need("v", "act", i_g2)
+        i_s = V(v.tensor_copy(T.vv[:, vb:vb + vw].indirect(T.en0[:, eb:eb + R]), T.g2[:, gb + 1:gb + w + 1]))
+        return i_e, i_s
+
+    def offsets(bt, bs, i_s):
+        out = []
+        need("v", "vec", i_s)
+        i1, i2 = [], []
+        for b in bs:
+            p, c = 128 * (PB[bt] + b), VB[bt] + 128 * b
+            i1.append(V(v.tensor_tensor_scan(T.la[:, p:p + 128], T.d0[:, c:c + 128], T.vv[:, c:c + 128],
+                                             T.g2[:, GB[bt] + 16 * b:GB[bt] + 16 * b + 1], A.add, A.max)))
+        for b, i in zip(bs, i1):
+            p = 128 * (PB[bt] + b)
+            need("v", "vec", i)
+            i2.append(V(v.tensor_tensor_scan(T.lb[:, p:p + 128], T.dmk[:], T.la[:, p:p + 128], 0.0, A.add, A.max)))
+        for b, i in zip(bs, i2):
+            t = PB[bt] + b
+            need("v", "vec", i)
+            out.append(V(v.tensor_scalar(T.off[:, 32 * t:32 * t + 32], T.lb[:, 128 * t + 3:128 * t + 128:4],
+                                         T.cst[:], None, A.add)))
+        return out
+
+    def win(t):
+        return T.xs[:, :].indirect(T.off[:, 32 * t:32 * t + 32])
+
+    def gather_s(t, i):
+        need("s", "lx", 16)
+        need("s", "vec", i)
+        return S(sc.activation(T.tile[:, 512 * t:512 * t + 512], win(t), F.Copy))
+
+    def gather_v(t, i):
+        need("v", "lx", 16)
+        need("v", "vec", i)
+        return V(v.tensor_copy(T.tile[:, 512 * t:512 * t + 512], win(t)))
+
+    def quant(t, sem, i):
+        need("v", sem, i)
+        return V(v.quantize_mx(T.qc[:, 128 * t:128 * t + 128], T.qp[:, 128 * t:128 * t + 128],
+                               T.tile[:, 512 * t:512 * t + 512]))
+
+    def codes(t):
+        return u8(T.qc[:, 128 * t:128 * t + 128])
+
+    def plane(t):
+        return T.qp[:, 128 * t:128 * t + 128]
+
+    n_same = sum(len(lane_same(topo, T.cores[own[j]], core, at(own[j]))) for j in range(1, 4))
+    n_hand = 4 * (len(topo.engines(hs[0], T.cores[oth[0]])) // 2)
+
+    def to_same(js, what, parts):
+        trs = []
+        for i, j in enumerate(js):
+            d, dc = own[j], T.cores[own[j]]
+            s = at(d) - 1
+            e = part(topo.engines(core, dc), i, parts)
+            if what == "c":
+                trs.append((dc, u8(T.lc[:, 128 * s:128 * s + 128]), codes(j - 1), "t%d" % s, e))
+            else:
+                trs.append((dc, T.lp[:, 128 * s:128 * s + 128], plane(j - 1), "t%d" % s, e))
+        fused(trs)
+
+    i_e, is_s = ends("S", 3, T.cds[:, 0:3], "cds", n_same)
+    need("g", "vec", i_e)
+    fused([(T.cores[own[j]], T.el[:, 2 * (at(own[j]) - 1):2 * at(own[j]) - 1], T.en0[:, j - 1:j], "ens",
+            lane_same(topo, core, T.cores[own[j]], j)) for j in range(1, 4)])
+    o = offsets("S", [0, 1], is_s)
+    i0 = gather_s(0, o[0])
+    i1 = gather_v(1, o[1])
+    quant(0, "act", i0)
+    i = quant(1, "vec", i1)
+    need("g", "vec", i)
+    to_same([1, 2], "c", 2)
+    to_same([1, 2], "p", 2)
+
+    i_e, i_s = ends("O", 4, T.cdo[:, 0:4], "cdo", n_hand)
+    need("g", "vec", i_e)
+    fused([(hs[k], T.hen[:, 0:1], T.en0[:, 4 + k:5 + k], "hen", lane_up(topo, core, hs[k], k)) for k in range(4)])
+    o = offsets("O", [0, 1], i_s)
+    i0, i1 = gather_s(3, o[0]), gather_s(4, o[1])
+    o = offsets("O", [2, 3], i_s)
+    i2 = gather_s(5, o[0])
+    quant(3, "act", i0)
+    i = quant(4, "act", i1)
+    need("g", "vec", i)
+    fused([(hs[k], u8(T.hc[:, 0:128]), codes(3 + k), "hc", part(topo.engines(core, hs[k]), k, 2)) for k in (0, 1)])
+    i3 = gather_v(6, o[1])
+    quant(5, "act", i2)
+    i = quant(6, "vec", i3)
+    need("g", "vec", i)
+    fused([(hs[k], u8(T.hc[:, 0:128]), codes(3 + k), "hc", part(topo.engines(core, hs[k]), k - 2, 2)) for k in (2, 3)])
+    fused([(hs[k], T.hp[:, 0:128], plane(3 + k), "hp", part(topo.engines(core, hs[k]), k, 4)) for k in range(4)])
+
+    o = offsets("S", [2], is_s)
+    i = quant(2, "act", gather_s(2, o[0]))
+    need("g", "vec", i)
+    to_same([3], "c", 1)
+    to_same([3], "p", 1)
+
+    i = V(v.tensor_copy(T.cdm[:, 0:1], T.cdu[:, rank:rank + 1]))
+    need("v", "vec", i)
+    need("s", "vec", i)
+    i_e, i_s = ends("M", 1, T.cdm[:, 0:1], None, 0)
+    o = offsets("M", [0], i_s)
+    i_own = quant(7, "act", gather_s(7, o[0]))
+    need("v", "lw", 16)
+    i_w = V(v.quantize_mx(T.wc[:], T.wp[:], T.ws[:]))
+
+    V(v.tensor_scalar(T.en[:, 14:15], T.s1[:, GB["M"] + 15:GB["M"] + 16], -1.0, None, A.add))
+
+    def last(lo, n, sem, val):
+        need("v", sem, val)
+        i = V(v.tensor_scalar(T.ea[:, lo:lo + n], T.el[:, 2 * lo:2 * (lo + n) - 1:2], -1.0, None, A.add))
+        need("v", "vec", i)
+        i = V(v.tensor_scalar(T.eb[:, lo:lo + n], T.ea[:, lo:lo + n], 127, None, A.bitwise_and))
+        need("v", "vec", i)
+        return V(v.tensor_copy(T.en[:, 2 * lo:2 * (lo + n) - 1:2], T.eb[:, lo:lo + n]))
+
+    def border(s):
+        return V(v.tensor_copy(T.mk[:, 136 * s + 8:136 * s + 136].indirect(T.en[:, 2 * s:2 * s + 1]), T.neg[:]))
+
+    i = last(0, 3, "ens", n_same)
+    need("v", "vec", i)
+    need("v", "act", i_mk)
+    brd = {s: border(s) for s in (2, 1, 7, 0)}
+
+    def tile_engines(s):
+        if s >= 3:
+            return 2 * len(topo.engines(hs[0], T.cores[oth[0]]))
+        e = len(topo.engines(T.cores[own[s + 1]], core))
+        j = (-(s + 1)) % 4
+        return 2 * (e // 2 if j < 3 else e)
+
+    def score(s):
+        ps = T.ps[:, 512 * s:512 * s + 128]
+        need("t", "vec", i_w)
+        if s == 7:
+            need("t", "vec", i_own)
+            i = done("pe", pe.matmul_mx(ps, T.wc[:], T.wp[:], T.qc[:, 896:1024], T.qp[:, 896:1024], True, True))
+            q = rank
+        else:
+            need("t", "t%d" % s, tile_engines(s))
+            i = done("pe", pe.matmul_mx(ps, T.wc[:], T.wp[:], T.lc[:, 128 * s:128 * s + 128],
+                                        T.lp[:, 128 * s:128 * s + 128], True, True))
+            q = own[s + 1] if s < 3 else oth[s - 3]
+        need("v", "pe", i)
+        need("v", "vec", brd[s])
+        i = V(v.tensor_tensor_scan(T.so[:, 128 * s:128 * s + 128], T.mk[:, 136 * s + 7:136 * s + 135], ps, -BIG, A.min, A.max))
+        need("s", "vec", i)
+        i = S(sc.activation(T.ys[:, 16 * q:16 * q + 16], T.so[:, 128 * s:128 * s + 128].indirect(T.en[:, 2 * s:2 * s + 1]), F.Copy))
+        need("y", "act", i)
+        g.sync.dma_start(T.y[:, 16 * q:16 * q + 16], T.ys[:, 16 * q:16 * q + 16]).then_inc(T.sem.ly, 16)
+
+    for s in (2, 1, 7):
+        score(s)
+    i = last(3, 4, "eno", n_hand)
+    need("v", "vec", i)
+    for s in (3, 6, 5, 4):
+        brd[s] = border(s)
+    score(0)
+    for s in (3, 6, 5, 4):
+        score(s)
+
+    for sem in ("vec", "act", "pe", "gc", "sent"):
+        need("g", sem, cnt[sem])
+    need("g", "ly", 128)

@@ -15,14 +15,14 @@ SCRATCH = {
     "stt": ("sbuf", [128, 64], "float32"), "lnt": ("sbuf", [128, 64], "float32"),
     "poi": ("sbuf", [128, 4], "int32"), "poa": ("sbuf", [128, 4], "int32"), "pou": ("sbuf", [128, 4], "uint16"),
     "pp": ("sbuf", [128, 1], "int32"), "ki": ("sbuf", [128, 3], "int32"), "kf": ("sbuf", [128, 3], "float32"),
-    "cst": ("sbuf", [128, 1], "float32"),
+    "cst": ("sbuf", [128, 1], "float32"), "zz": ("sbuf", [128, 1096], "bfloat16"),
     "ii": ("sbuf", [128, 64], "float32"), "jj": ("sbuf", [128, 128], "float32"),
     "le": ("sbuf", [128, 64], "float32"), "dmb": ("sbuf", [128, 128], "float32"), "dmk": ("sbuf", [128, 128], "float32"),
     "rst": ("sbuf", [128, 64], "float32"), "far": ("sbuf", [128, 64], "float32"), "neg": ("sbuf", [128, 16], "float32"),
     "cds": ("sbuf", [128, 4], "uint16"), "cdo": ("sbuf", [128, 4], "uint16"),
     "g1": ("sbuf", [128, 152], "float32"), "s1": ("sbuf", [128, 152], "float32"), "g2": ("sbuf", [128, 152], "float32"),
     "en0": ("sbuf", [128, 16], "uint16"),
-    "vv": ("sbuf", [128, 1096], "float32"), "d0": ("sbuf", [128, 1048], "float32"),
+    "vv": ("sbuf", [128, 1048], "float32"), "d0": ("sbuf", [128, 1048], "float32"),
     "la": ("sbuf", [128, 1024], "float32"), "lb": ("sbuf", [128, 1024], "float32"),
     "off": ("sbuf", [128, 256], "uint16"),
     "xs": ("sbuf", [128, 4 * (TOK + CAP)], "bfloat16"), "ws": ("sbuf", [128, 512], "bfloat16"),
@@ -71,8 +71,18 @@ def lane_up(topo, c, h, k):
     return part(e[len(e) // 2:], k, 4)
 
 
+def codes_up(topo, c, h, k):
+    e = topo.engines(c, h)
+    return part(e[len(e) // 2:], k, 2) if k < 2 else part(e, k - 2, 2)
+
+
 def lane_same(topo, c, d, j):
     return part(topo.engines(c, d), j - 1, 4)
+
+
+def tile_same(topo, c, d, j):
+    e = topo.engines(c, d)
+    return part(e, j - 1, 4) if j < 3 else part(e, 1, 2)
 
 
 def u8(ap):
@@ -98,7 +108,7 @@ def hand_on(g, core, T, topo, r, k):
     g.wait_ge(T.sem.hen, n_up)
     on(T.el[:, 6 + 2 * slot:7 + 2 * slot], T.hen[:, 0:1], "eno", part(e, 1, 2))
     s = 3 + slot
-    g.wait_ge(T.sem.hc, len(topo.engines(rc, core)) // 2)
+    g.wait_ge(T.sem.hc, len(codes_up(topo, rc, core, k)))
     on(u8(T.lc[:, 128 * s:128 * s + 128]), u8(T.hc[:, 0:128]), "t%d" % s, e)
     g.wait_ge(T.sem.hp, len(topo.engines(rc, core)) // 4)
     on(T.lp[:, 128 * s:128 * s + 128], T.hp[:, 0:128], "t%d" % s, e)
@@ -145,14 +155,28 @@ def rank_program(g, core, T, topo):
     sc.dma_start(T.ws[:], T.qw[:]).then_inc(T.sem.lw, 16)
 
     done("gc", g.iota(T.pp[:], [[0, 1]], 0, 1))
-    done("gc", g.iota(T.poi[:], [[1, 4]], 0, 4))
+    i_io = done("gc", g.iota(T.poi[:], [[1, 4]], 0, 4))
     done("gc", g.iota(T.ii[:], [[0, 4], [1, 16]], 0, 0, allow_small_or_imprecise_dtypes=True))
     done("gc", g.iota(T.jj[:], [[0, 32], [1, 4]], 0, 0, allow_small_or_imprecise_dtypes=True))
 
-    i_z = V(v.memset(T.vv[:], 0.0))
+    i_z = V(v.memset(T.zz[:], 0.0))
     need("s", "vec", i_z)
-    i_d0 = S(sc.activation(T.d0[:], T.vv[:, 0:1048], F.Copy, bias=4.0))
-    i_mk = S(sc.activation(T.mk[:], T.vv[:], F.Copy, bias=BIG))
+    i_d0 = S(sc.activation(T.d0[:], T.zz[:, 0:1048], F.Copy, bias=4.0))
+    i_vv = S(sc.activation(T.vv[:], T.zz[:, 0:1048], F.Copy))
+    i_mk = S(sc.activation(T.mk[:], T.zz[:], F.Copy, bias=BIG))
+    V(v.memset(T.g2[:], 0.0))
+    V(v.memset(T.far[:], -FAR))
+    V(v.memset(T.neg[:], -BIG))
+    V(v.memset(T.rst[:], 0.0))
+    need("v", "gc", i_io)
+    V(v.tensor_scalar(T.ki[:, 0:1], T.pp[:], 15, None, A.bitwise_and))
+    V(v.tensor_scalar(T.ki[:, 1:2], T.pp[:], 3, None, A.bitwise_and))
+    i_k = V(v.tensor_scalar(T.ki[:, 2:3], T.pp[:], 15, 2, A.bitwise_and, A.arith_shift_right))
+    i_p = V(v.tensor_scalar(T.poa[:], T.poi[:], 63, None, A.bitwise_and))
+    need("v", "vec", i_k)
+    V(v.tensor_copy(T.kf[:], T.ki[:]))
+    need("v", "vec", i_p)
+    V(v.tensor_copy(T.pou[:], T.poa[:]))
 
     need("v", "lcd", 128)
     i_cd = V(v.tensor_copy(T.cdu[:], T.cdi[:]))
@@ -176,26 +200,15 @@ def rank_program(g, core, T, topo):
     need("g", "ltab", 32)
     i_tab = done("gc", g.partition_broadcast(T.tab[:], T.row[0:1, :], 128))
 
-    V(v.memset(T.g2[:], 0.0))
-    V(v.memset(T.far[:], -FAR))
-    V(v.memset(T.neg[:], -BIG))
-    V(v.memset(T.xs[:, 4 * TOK:], 0.0))
-    i_r = V(v.memset(T.rst[:], 0.0))
-    need("v", "gc", 4)
-    V(v.tensor_scalar(T.ki[:, 0:1], T.pp[:], 15, None, A.bitwise_and))
-    V(v.tensor_scalar(T.ki[:, 1:2], T.pp[:], 3, None, A.bitwise_and))
-    i_k = V(v.tensor_scalar(T.ki[:, 2:3], T.pp[:], 15, 2, A.bitwise_and, A.arith_shift_right))
-    i_p = V(v.tensor_scalar(T.poa[:], T.poi[:], 63, None, A.bitwise_and))
-    need("v", "vec", i_k)
-    i_k = V(v.tensor_copy(T.kf[:], T.ki[:]))
-    need("v", "vec", i_p)
-    i_p = V(v.tensor_copy(T.pou[:], T.poa[:]))
+    need("v", "vec", i_cd)
+    V(v.tensor_copy(T.cdm[:, 0:1], T.cdu[:, rank:rank + 1]))
     for b in range(1, 4):
         V(v.memset(T.rst[:, 16 * b:16 * b + 1], 128.0 * b))
-    need("v", "vec", i_k)
+    need("v", "gc", 4)
     V(v.tensor_scalar(T.le[:], T.ii[:], T.kf[:, 0:1], None, A.is_le))
     i_m = V(v.tensor_scalar(T.dmb[:], T.jj[:], T.kf[:, 2:3], FAR + LIFT, A.is_gt, A.mult))
     V(v.tensor_scalar(T.cst[:], T.kf[:, 2:3], -3.0, LIFT, A.add, A.mult))
+    V(v.memset(T.xs[:, 4 * TOK:], 0.0))
     need("v", "vec", i_m)
     V(v.tensor_scalar(T.dmk[:], T.dmb[:], -FAR, None, A.add))
     need("v", "act", i_d0)
@@ -203,29 +216,34 @@ def rank_program(g, core, T, topo):
     V(v.memset(T.d0[:, 392:904:128], 0.0))
     V(v.memset(T.d0[:, 912:913], 0.0))
     need("v", "gc", i_tab)
-    need("v", "vec", i_p)
     V(v.tensor_copy(T.stt[:], T.tab[:, 0:64].indirect(T.pou[:, 0:4])))
     i_ln = V(v.tensor_copy(T.lnt[:], T.tab[:, 64:128].indirect(T.pou[:, 0:4])))
 
-    def ends(bt, R, off, sem, val):
-        gb, eb, vb, vw = GB[bt], EB[bt], VB[bt], VW[bt]
+    def ends(bt, R, off, on_s):
+        gb, eb = GB[bt], EB[bt]
         w = 16 * R
-        if sem:
-            need("v", sem, val)
-            need("s", sem, val)
         need("v", "vec", i_ln)
-        need("s", "vec", i_ln)
-        i_g2 = S(sc.activation(T.g2[:, gb:gb + w], T.stt[:, 0:64].indirect(off), F.Identity, bias=T.kf[:, 1:2], scale=4.0))
+        if on_s:
+            need("s", "vec", i_ln)
+            st = ("act", S(sc.activation(T.g2[:, gb:gb + w], T.stt[:, 0:64].indirect(off), F.Identity,
+                                         bias=T.kf[:, 1:2], scale=4.0)))
         i = V(v.tensor_tensor(T.g1[:, gb:gb + w], T.lnt[:, 0:64].indirect(off), T.le[:, 0:w], A.mult))
+        if not on_s:
+            st = ("vec", V(v.tensor_scalar(T.g2[:, gb:gb + w], T.stt[:, 0:64].indirect(off), 4.0, T.kf[:, 1:2],
+                                           A.mult, A.add)))
         need("v", "vec", i)
         i = V(v.tensor_tensor_scan(T.s1[:, gb:gb + w], T.rst[:, 0:w], T.g1[:, gb:gb + w], 0.0, A.max, A.add))
         need("v", "vec", i)
-        i_e = V(v.tensor_copy(T.en0[:, eb:eb + R], T.s1[:, gb + 15:gb + w:16]))
+        return V(v.tensor_copy(T.en0[:, eb:eb + R], T.s1[:, gb + 15:gb + w:16])), st
+
+    def scatter(bt, R, i_e, st):
+        gb, e, vb, vw = GB[bt], EB[bt], VB[bt], VW[bt]
         need("v", "vec", i_e)
-        V(v.tensor_copy(T.d0[:, vb:vb + vw].indirect(T.en0[:, eb:eb + R]), T.far[:, 0:w]))
-        need("v", "act", i_g2)
-        i_s = V(v.tensor_copy(T.vv[:, vb:vb + vw].indirect(T.en0[:, eb:eb + R]), T.g2[:, gb + 1:gb + w + 1]))
-        return i_e, i_s
+        need("v", "act", i_vv)
+        where = T.en0[:, e:e + R]
+        V(v.tensor_copy(T.d0[:, vb:vb + vw].indirect(where), T.far[:, 0:16 * R]))
+        need("v", *st)
+        return V(v.tensor_copy(T.vv[:, vb:vb + vw].indirect(where), T.g2[:, gb + 1:gb + 16 * R + 1]))
 
     def offsets(bt, bs, i_s):
         out = []
@@ -273,64 +291,51 @@ def rank_program(g, core, T, topo):
     n_same = sum(len(lane_same(topo, T.cores[own[j]], core, at(own[j]))) for j in range(1, 4))
     n_hand = 4 * (len(topo.engines(hs[0], T.cores[oth[0]])) // 2)
 
-    def to_same(js, what, parts):
-        trs = []
-        for i, j in enumerate(js):
-            d, dc = own[j], T.cores[own[j]]
-            s = at(d) - 1
-            e = part(topo.engines(core, dc), i, parts)
-            if what == "c":
-                trs.append((dc, u8(T.lc[:, 128 * s:128 * s + 128]), codes(j - 1), "t%d" % s, e))
-            else:
-                trs.append((dc, T.lp[:, 128 * s:128 * s + 128], plane(j - 1), "t%d" % s, e))
-        fused(trs)
+    i_e, st = ends("M", 1, T.cdm[:, 0:1], False)
+    i7 = gather_s(7, offsets("M", [0], scatter("M", 1, i_e, st))[0])
 
-    i_e, is_s = ends("S", 3, T.cds[:, 0:3], "cds", n_same)
+    need("v", "cds", n_same)
+    i_e, st = ends("S", 3, T.cds[:, 0:3], False)
     need("g", "vec", i_e)
     fused([(T.cores[own[j]], T.el[:, 2 * (at(own[j]) - 1):2 * at(own[j]) - 1], T.en0[:, j - 1:j], "ens",
             lane_same(topo, core, T.cores[own[j]], j)) for j in range(1, 4)])
-    o = offsets("S", [0, 1], is_s)
-    i0 = gather_s(0, o[0])
-    i1 = gather_v(1, o[1])
+    i_s = scatter("S", 3, i_e, st)
+    i0 = gather_s(0, offsets("S", [0], i_s)[0])
+    o = offsets("S", [1, 2], i_s)
+    i2 = gather_s(2, o[1])
+    i1 = gather_v(1, o[0])
     quant(0, "act", i0)
-    i = quant(1, "vec", i1)
+    quant(1, "vec", i1)
+    i = quant(2, "act", i2)
     need("g", "vec", i)
-    to_same([1, 2], "c", 2)
-    to_same([1, 2], "p", 2)
+    to = [(T.cores[own[j]], at(own[j]) - 1, j) for j in range(1, 4)]
+    fused([(dc, u8(T.lc[:, 128 * s:128 * s + 128]), codes(j - 1), "t%d" % s, tile_same(topo, core, dc, j)) for dc, s, j in to])
+    fused([(dc, T.lp[:, 128 * s:128 * s + 128], plane(j - 1), "t%d" % s, tile_same(topo, core, dc, j)) for dc, s, j in to])
 
-    i_e, i_s = ends("O", 4, T.cdo[:, 0:4], "cdo", n_hand)
+    need("v", "cdo", n_hand)
+    need("s", "cdo", n_hand)
+    i_e, st = ends("O", 4, T.cdo[:, 0:4], True)
     need("g", "vec", i_e)
     fused([(hs[k], T.hen[:, 0:1], T.en0[:, 4 + k:5 + k], "hen", lane_up(topo, core, hs[k], k)) for k in range(4)])
-    o = offsets("O", [0, 1], i_s)
-    i0, i1 = gather_s(3, o[0]), gather_s(4, o[1])
+    i_s = scatter("O", 4, i_e, st)
+    i3 = gather_s(3, offsets("O", [0], i_s)[0])
+    i4 = gather_s(4, offsets("O", [1], i_s)[0])
     o = offsets("O", [2, 3], i_s)
-    i2 = gather_s(5, o[0])
-    quant(3, "act", i0)
-    i = quant(4, "act", i1)
+    i5 = gather_s(5, o[0])
+    quant(3, "act", i3)
+    i = quant(4, "act", i4)
     need("g", "vec", i)
-    fused([(hs[k], u8(T.hc[:, 0:128]), codes(3 + k), "hc", part(topo.engines(core, hs[k]), k, 2)) for k in (0, 1)])
-    i3 = gather_v(6, o[1])
-    quant(5, "act", i2)
-    i = quant(6, "vec", i3)
+    fused([(hs[k], u8(T.hc[:, 0:128]), codes(3 + k), "hc", codes_up(topo, core, hs[k], k)) for k in (0, 1)])
+    i6 = gather_v(6, o[1])
+    quant(5, "act", i5)
+    i = quant(6, "vec", i6)
     need("g", "vec", i)
-    fused([(hs[k], u8(T.hc[:, 0:128]), codes(3 + k), "hc", part(topo.engines(core, hs[k]), k - 2, 2)) for k in (2, 3)])
+    fused([(hs[k], u8(T.hc[:, 0:128]), codes(3 + k), "hc", codes_up(topo, core, hs[k], k)) for k in (2, 3)])
     fused([(hs[k], T.hp[:, 0:128], plane(3 + k), "hp", part(topo.engines(core, hs[k]), k, 4)) for k in range(4)])
 
-    o = offsets("S", [2], is_s)
-    i = quant(2, "act", gather_s(2, o[0]))
-    need("g", "vec", i)
-    to_same([3], "c", 1)
-    to_same([3], "p", 1)
-
-    i = V(v.tensor_copy(T.cdm[:, 0:1], T.cdu[:, rank:rank + 1]))
-    need("v", "vec", i)
-    need("s", "vec", i)
-    i_e, i_s = ends("M", 1, T.cdm[:, 0:1], None, 0)
-    o = offsets("M", [0], i_s)
-    i_own = quant(7, "act", gather_s(7, o[0]))
+    i_own = quant(7, "act", i7)
     need("v", "lw", 16)
     i_w = V(v.quantize_mx(T.wc[:], T.wp[:], T.ws[:]))
-
     V(v.tensor_scalar(T.en[:, 14:15], T.s1[:, GB["M"] + 15:GB["M"] + 16], -1.0, None, A.add))
 
     def last(lo, n, sem, val):
@@ -347,14 +352,13 @@ def rank_program(g, core, T, topo):
     i = last(0, 3, "ens", n_same)
     need("v", "vec", i)
     need("v", "act", i_mk)
-    brd = {s: border(s) for s in (2, 1, 7, 0)}
+    brd = {s: border(s) for s in (7, 2, 1, 0)}
 
     def tile_engines(s):
         if s >= 3:
             return 2 * len(topo.engines(hs[0], T.cores[oth[0]]))
-        e = len(topo.engines(T.cores[own[s + 1]], core))
         j = (-(s + 1)) % 4
-        return 2 * (e // 2 if j < 3 else e)
+        return 2 * len(tile_same(topo, T.cores[own[s + 1]], core, j))
 
     def score(s):
         ps = T.ps[:, 512 * s:512 * s + 128]
@@ -376,13 +380,12 @@ def rank_program(g, core, T, topo):
         need("y", "act", i)
         g.sync.dma_start(T.y[:, 16 * q:16 * q + 16], T.ys[:, 16 * q:16 * q + 16]).then_inc(T.sem.ly, 16)
 
-    for s in (2, 1, 7):
+    for s in (7, 2, 1, 0):
         score(s)
     i = last(3, 4, "eno", n_hand)
     need("v", "vec", i)
     for s in (3, 6, 5, 4):
         brd[s] = border(s)
-    score(0)
     for s in (3, 6, 5, 4):
         score(s)
 

@@ -3,26 +3,28 @@ from concourse.mybir import dt, AluOpType as A, ActivationFunctionType as F
 
 N, TOK, CAP = 8, 512, 128
 BIG, FAR, LIFT = 1.0e29, 1.0e6, 4096.0
-VB = {"S": 0, "O": 392, "M": 912}
-VW = {"S": 392, "O": 520, "M": 136}
+WB = 136
+VB = {"S": 0, "O": 408, "M": 952}
 GB = {"S": 0, "O": 56, "M": 128}
 EB = {"S": 0, "O": 4, "M": 8}
 PB = {"S": 0, "O": 3, "M": 7}
+CARRY = {0: (0, 3), 1: (1, 2)}
 
 SCRATCH = {
     "cdi": ("sbuf", [128, 8], "int32"), "cdu": ("sbuf", [128, 8], "uint16"), "cdm": ("sbuf", [128, 2], "uint16"),
     "row": ("sbuf", [1, 128], "int32"), "tab": ("sbuf", [128, 128], "int32"),
     "stt": ("sbuf", [128, 64], "float32"), "lnt": ("sbuf", [128, 64], "float32"),
+    "nes": ("sbuf", [128, 64], "float32"), "nen": ("sbuf", [128, 64], "float32"),
     "poi": ("sbuf", [128, 4], "int32"), "poa": ("sbuf", [128, 4], "int32"), "pou": ("sbuf", [128, 4], "uint16"),
     "pp": ("sbuf", [128, 1], "int32"), "ki": ("sbuf", [128, 3], "int32"), "kf": ("sbuf", [128, 3], "float32"),
-    "cst": ("sbuf", [128, 1], "float32"), "zz": ("sbuf", [128, 1096], "bfloat16"),
+    "csu": ("sbuf", [128, 1], "float32"), "cst": ("sbuf", [128, 1], "float32"), "zz": ("sbuf", [128, 1032], "bfloat16"),
     "ii": ("sbuf", [128, 64], "float32"), "jj": ("sbuf", [128, 128], "float32"),
     "le": ("sbuf", [128, 64], "float32"), "dmb": ("sbuf", [128, 128], "float32"), "dmk": ("sbuf", [128, 128], "float32"),
-    "rst": ("sbuf", [128, 64], "float32"), "far": ("sbuf", [128, 64], "float32"), "neg": ("sbuf", [128, 16], "float32"),
+    "rst": ("sbuf", [128, 64], "float32"), "fr": ("sbuf", [128, 128], "float32"), "neg": ("sbuf", [128, 64], "float32"),
     "cds": ("sbuf", [128, 4], "uint16"), "cdo": ("sbuf", [128, 4], "uint16"),
     "g1": ("sbuf", [128, 152], "float32"), "s1": ("sbuf", [128, 152], "float32"), "g2": ("sbuf", [128, 152], "float32"),
-    "en0": ("sbuf", [128, 16], "uint16"),
-    "vv": ("sbuf", [128, 1048], "float32"), "d0": ("sbuf", [128, 1048], "float32"),
+    "dl": ("sbuf", [128, 152], "float32"), "en0": ("sbuf", [128, 16], "uint16"),
+    "vv": ("sbuf", [128, 1088], "float32"),
     "la": ("sbuf", [128, 1024], "float32"), "lb": ("sbuf", [128, 1024], "float32"),
     "off": ("sbuf", [128, 256], "uint16"),
     "xs": ("sbuf", [128, 4 * (TOK + CAP)], "bfloat16"), "ws": ("sbuf", [128, 512], "bfloat16"),
@@ -30,15 +32,14 @@ SCRATCH = {
     "qc": ("sbuf", [128, 1024], "float8_e4m3fn_x4"), "qp": ("sbuf", [128, 1024], "uint8"),
     "wc": ("sbuf", [128, 128], "float8_e4m3fn_x4"), "wp": ("sbuf", [128, 128], "uint8"),
     "lc": ("sbuf", [128, 896], "float8_e4m3fn_x4"), "lp": ("sbuf", [128, 896], "uint8"),
-    "el": ("sbuf", [128, 16], "uint16"), "ea": ("sbuf", [128, 8], "int32"), "eb": ("sbuf", [128, 8], "int32"),
-    "en": ("sbuf", [128, 16], "uint16"),
-    "mk": ("sbuf", [128, 1096], "float32"), "so": ("sbuf", [128, 1024], "float32"), "ys": ("sbuf", [128, 128], "float32"),
+    "el": ("sbuf", [128, 8], "float32"), "ef": ("sbuf", [128, 12], "float32"), "en": ("sbuf", [128, 12], "uint16"),
+    "mk": ("sbuf", [128, 1032], "float32"), "so": ("sbuf", [128, 1024], "float32"), "ys": ("sbuf", [128, 128], "float32"),
     "ps": ("psum", [128, 4096], "float32"),
-    "hcd": ("sbuf", [128, 2], "uint16"), "hen": ("sbuf", [128, 2], "uint16"),
-    "hc": ("sbuf", [128, 128], "float8_e4m3fn_x4"), "hp": ("sbuf", [128, 128], "uint8"),
+    "hcd": ("sbuf", [128, 8], "uint16"), "hen": ("sbuf", [128, 1], "float32"),
+    "hc": ("sbuf", [128, 128], "float8_e4m3fn_x4"), "hp": ("sbuf", [128, 256], "uint8"),
 }
 SEMAPHORES = (["vec", "act", "pe", "gc", "lcd", "ltab", "lx", "lw", "ly", "sent", "cds", "cdo", "ens", "eno",
-               "hcd", "hen", "hc", "hp"] + ["t%d" % s for s in range(7)])
+               "hcd", "hen", "hc", "hp", "hq"] + ["t%d" % s for s in range(7)])
 
 
 def groups(T, topo, r):
@@ -54,7 +55,7 @@ def helpers(T, topo, r):
     hs = [h for h in topo.cores_of(c) if h != c and topo.may_write(h, dst)]
     near = [h for h in hs if topo.die(h) == topo.die(c)]
     far = [h for h in hs if topo.die(h) != topo.die(c)]
-    return [near[0], far[0], far[1], near[1]]
+    return [near[0], far[0], near[1], far[1]]
 
 
 def part(e, i, n):
@@ -66,21 +67,37 @@ def bits(e):
     return sum(1 << x for x in e)
 
 
-def lane_up(topo, c, h, k):
+def upper(topo, c, h):
     e = topo.engines(c, h)
-    return part(e[len(e) // 2:], k, 4)
+    return e[len(e) // 2:]
+
+
+def lists_up(topo, c, h, k):
+    return part(upper(topo, c, h), k, 2)
+
+
+def ends_up(topo, c, h, k):
+    return part(upper(topo, c, h), k, 4)
 
 
 def codes_up(topo, c, h, k):
-    e = topo.engines(c, h)
-    return part(e[len(e) // 2:], k, 2) if k < 2 else part(e, k - 2, 2)
+    return part(upper(topo, c, h), k, 2) if k in CARRY else part(topo.engines(c, h), k - 2, 2)
+
+
+def plane_up(topo, c, h, k):
+    return part(topo.engines(c, h), k, 4) if k in CARRY else part(topo.engines(c, h), k - 2, 2)
 
 
 def lane_same(topo, c, d, j):
     return part(topo.engines(c, d), j - 1, 4)
 
 
-def tile_same(topo, c, d, j):
+def codes_same(topo, c, d, j):
+    e = topo.engines(c, d)
+    return part(e, j - 1, 2) if j < 3 else e
+
+
+def plane_same(topo, c, d, j):
     e = topo.engines(c, d)
     return part(e, j - 1, 4) if j < 3 else part(e, 1, 2)
 
@@ -91,27 +108,41 @@ def u8(ap):
 
 def hand_on(g, core, T, topo, r, k):
     _, oth, a = groups(T, topo, r)
-    d = oth[k]
-    dc, rc = T.cores[d], T.cores[r]
-    slot = (a - groups(T, topo, d)[2]) % 4
-    rid, pid = topo.addr(dc, core)
-    e = topo.engines(core, dc)
-    n_up = len(lane_up(topo, rc, core, k))
+    rc = T.cores[r]
     sent = [0]
 
-    def on(dst, src, sem, eng):
+    def slot(n):
+        return (a - groups(T, topo, oth[n])[2]) % 4
+
+    def to(n):
+        return T.cores[oth[n]]
+
+    def on(n, dst, src, sem, eng):
+        rid, pid = topo.addr(to(n), core)
         g.remote_dma(dst, src, T.sem[sem], T.sem.sent, pid, rid, bits(eng))
         sent[0] += len(eng)
 
-    g.wait_ge(T.sem.hcd, n_up)
-    on(T.cdo[:, slot:slot + 1], T.hcd[:, 0:1], "cdo", part(e, 0, 2))
-    g.wait_ge(T.sem.hen, n_up)
-    on(T.el[:, 6 + 2 * slot:7 + 2 * slot], T.hen[:, 0:1], "eno", part(e, 1, 2))
-    s = 3 + slot
+    if k in CARRY:
+        g.wait_ge(T.sem.hcd, len(lists_up(topo, rc, core, k)))
+        ts = []
+        for i, n in enumerate(CARRY[k]):
+            rid, pid = topo.addr(to(n), core)
+            e = part(topo.engines(core, to(n)), i, 2)
+            ts.append(RemoteDMATransfer(dst_ids=[DstId(rid=rid, pnc=pid)], dma_engine_mask=bits(e), remote_sem=T.sem.cdo,
+                                        src=T.hcd[:, oth[n]:oth[n] + 1], dst=T.cdo[:, slot(n):slot(n) + 1]))
+            sent[0] += len(e)
+        g.remote_dma_fused(ts, local_sem=T.sem.sent)
+    e = topo.engines(core, to(k))
+    g.wait_ge(T.sem.hen, len(ends_up(topo, rc, core, k)))
+    on(k, T.el[:, 3 + slot(k):4 + slot(k)], T.hen[:, 0:1], "eno", e)
+    s = 3 + slot(k)
     g.wait_ge(T.sem.hc, len(codes_up(topo, rc, core, k)))
-    on(u8(T.lc[:, 128 * s:128 * s + 128]), u8(T.hc[:, 0:128]), "t%d" % s, e)
-    g.wait_ge(T.sem.hp, len(topo.engines(rc, core)) // 4)
-    on(T.lp[:, 128 * s:128 * s + 128], T.hp[:, 0:128], "t%d" % s, e)
+    on(k, u8(T.lc[:, 128 * s:128 * s + 128]), u8(T.hc[:, 0:128]), "t%d" % s, e)
+    if k in CARRY:
+        for i, n in enumerate(CARRY[k]):
+            s = 3 + slot(n)
+            g.wait_ge(T.sem["hp" if i == 0 else "hq"], len(plane_up(topo, rc, core, n)))
+            on(n, T.lp[:, 128 * s:128 * s + 128], T.hp[:, 128 * i:128 * i + 128], "t%d" % s, topo.engines(core, to(n)))
     g.wait_ge(T.sem.sent, sent[0])
 
 
@@ -161,22 +192,17 @@ def rank_program(g, core, T, topo):
 
     i_z = V(v.memset(T.zz[:], 0.0))
     need("s", "vec", i_z)
-    i_d0 = S(sc.activation(T.d0[:], T.zz[:, 0:1048], F.Copy, bias=4.0))
-    i_vv = S(sc.activation(T.vv[:], T.zz[:, 0:1048], F.Copy))
+    i_vv = {}
+    for bt, R in (("S", 3), ("O", 4), ("M", 1)):
+        i_vv[bt] = S(sc.activation(T.vv[:, VB[bt]:VB[bt] + WB * R], T.zz[:, 0:WB * R], F.Copy))
+    i_fr = S(sc.activation(T.fr[:], T.zz[:, 0:128], F.Copy, bias=4.0))
+    S(sc.activation(T.neg[:], T.zz[:, 0:64], F.Copy, bias=-BIG))
     i_mk = S(sc.activation(T.mk[:], T.zz[:], F.Copy, bias=BIG))
-    V(v.memset(T.g2[:], 0.0))
-    V(v.memset(T.far[:], -FAR))
-    V(v.memset(T.neg[:], -BIG))
-    V(v.memset(T.rst[:], 0.0))
     need("v", "gc", i_io)
     V(v.tensor_scalar(T.ki[:, 0:1], T.pp[:], 15, None, A.bitwise_and))
     V(v.tensor_scalar(T.ki[:, 1:2], T.pp[:], 3, None, A.bitwise_and))
-    i_k = V(v.tensor_scalar(T.ki[:, 2:3], T.pp[:], 15, 2, A.bitwise_and, A.arith_shift_right))
+    V(v.tensor_scalar(T.ki[:, 2:3], T.pp[:], 15, 2, A.bitwise_and, A.arith_shift_right))
     i_p = V(v.tensor_scalar(T.poa[:], T.poi[:], 63, None, A.bitwise_and))
-    need("v", "vec", i_k)
-    V(v.tensor_copy(T.kf[:], T.ki[:]))
-    need("v", "vec", i_p)
-    V(v.tensor_copy(T.pou[:], T.poa[:]))
 
     need("v", "lcd", 128)
     i_cd = V(v.tensor_copy(T.cdu[:], T.cdi[:]))
@@ -194,75 +220,74 @@ def rank_program(g, core, T, topo):
     def at(d):
         return (a - groups(T, topo, d)[2]) % 4
 
-    fused([(hs[k], T.hcd[:, 0:1], T.cdu[:, oth[k]:oth[k] + 1], "hcd", lane_up(topo, core, hs[k], k)) for k in range(4)])
     fused([(T.cores[own[j]], T.cds[:, at(own[j]) - 1:at(own[j])], T.cdu[:, own[j]:own[j] + 1], "cds",
             lane_same(topo, core, T.cores[own[j]], j)) for j in range(1, 4)])
+    fused([(hs[k], T.hcd[:, 0:8], T.cdu[:, 0:8], "hcd", lists_up(topo, core, hs[k], k)) for k in CARRY])
     need("g", "ltab", 32)
     i_tab = done("gc", g.partition_broadcast(T.tab[:], T.row[0:1, :], 128))
 
-    need("v", "vec", i_cd)
-    V(v.tensor_copy(T.cdm[:, 0:1], T.cdu[:, rank:rank + 1]))
-    for b in range(1, 4):
-        V(v.memset(T.rst[:, 16 * b:16 * b + 1], 128.0 * b))
+    need("v", "vec", i_p)
+    V(v.tensor_copy(T.kf[:], T.ki[:]))
+    i_k = V(v.tensor_copy(T.pou[:], T.poa[:]))
+    i_r = V(v.memset(T.rst[:], 0.0))
     need("v", "gc", 4)
+    need("v", "vec", i_k)
     V(v.tensor_scalar(T.le[:], T.ii[:], T.kf[:, 0:1], None, A.is_le))
     i_m = V(v.tensor_scalar(T.dmb[:], T.jj[:], T.kf[:, 2:3], FAR + LIFT, A.is_gt, A.mult))
-    V(v.tensor_scalar(T.cst[:], T.kf[:, 2:3], -3.0, LIFT, A.add, A.mult))
-    V(v.memset(T.xs[:, 4 * TOK:], 0.0))
+    i_c = V(v.tensor_scalar(T.csu[:], T.kf[:, 2:3], -3.0, LIFT, A.add, A.mult))
+    need("v", "vec", i_r)
+    for b in range(1, 4):
+        V(v.memset(T.rst[:, 16 * b:16 * b + 1], float(WB * b)))
     need("v", "vec", i_m)
     V(v.tensor_scalar(T.dmk[:], T.dmb[:], -FAR, None, A.add))
-    need("v", "act", i_d0)
-    V(v.memset(T.d0[:, 0:384:128], 0.0))
-    V(v.memset(T.d0[:, 392:904:128], 0.0))
-    V(v.memset(T.d0[:, 912:913], 0.0))
+    need("v", "vec", i_c)
+    V(v.tensor_scalar(T.cst[:], T.csu[:], T.kf[:, 1:2], -4.0, A.add, A.add))
+    V(v.memset(T.g2[:], 0.0))
+    V(v.memset(T.xs[:, 4 * TOK:], 0.0))
     need("v", "gc", i_tab)
-    V(v.tensor_copy(T.stt[:], T.tab[:, 0:64].indirect(T.pou[:, 0:4])))
     i_ln = V(v.tensor_copy(T.lnt[:], T.tab[:, 64:128].indirect(T.pou[:, 0:4])))
+    i_st = V(v.tensor_scalar(T.stt[:], T.tab[:, 0:64].indirect(T.pou[:, 0:4]), 4.0, None, A.mult))
+    need("v", "vec", i_ln)
+    i = V(v.tensor_scalar(T.nes[:], T.lnt[:], -4.0, None, A.mult))
+    need("v", "vec", i)
+    i_ne = V(v.tensor_tensor(T.nen[:], T.nes[:], T.stt[:], A.subtract))
 
-    def ends(bt, R, off, on_s):
-        gb, eb = GB[bt], EB[bt]
+    def ends(bt, R, off, on_s, fill=None):
+        gb, eb, vb = GB[bt], EB[bt], VB[bt]
         w = 16 * R
-        need("v", "vec", i_ln)
+        need("v", "vec", i_ne)
         if on_s:
-            need("s", "vec", i_ln)
-            st = ("act", S(sc.activation(T.g2[:, gb:gb + w], T.stt[:, 0:64].indirect(off), F.Identity,
-                                         bias=T.kf[:, 1:2], scale=4.0)))
+            need("s", "vec", i_st)
+            st = ("act", S(sc.activation(T.g2[:, gb:gb + w], T.stt[:, 0:64].indirect(off), F.Copy)))
         i = V(v.tensor_tensor(T.g1[:, gb:gb + w], T.lnt[:, 0:64].indirect(off), T.le[:, 0:w], A.mult))
         if not on_s:
-            st = ("vec", V(v.tensor_scalar(T.g2[:, gb:gb + w], T.stt[:, 0:64].indirect(off), 4.0, T.kf[:, 1:2],
-                                           A.mult, A.add)))
+            st = ("vec", V(v.tensor_copy(T.g2[:, gb:gb + w], T.stt[:, 0:64].indirect(off))))
         need("v", "vec", i)
-        i = V(v.tensor_tensor_scan(T.s1[:, gb:gb + w], T.rst[:, 0:w], T.g1[:, gb:gb + w], 0.0, A.max, A.add))
-        need("v", "vec", i)
-        return V(v.tensor_copy(T.en0[:, eb:eb + R], T.s1[:, gb + 15:gb + w:16])), st
-
-    def scatter(bt, R, i_e, st):
-        gb, e, vb, vw = GB[bt], EB[bt], VB[bt], VW[bt]
-        need("v", "vec", i_e)
-        need("v", "act", i_vv)
-        where = T.en0[:, e:e + R]
-        V(v.tensor_copy(T.d0[:, vb:vb + vw].indirect(where), T.far[:, 0:16 * R]))
+        i_n = V(v.tensor_tensor_scan(T.s1[:, gb:gb + w], T.rst[:, 0:w], T.g1[:, gb:gb + w], 0.0, A.max, A.add))
         need("v", *st)
-        return V(v.tensor_copy(T.vv[:, vb:vb + vw].indirect(where), T.g2[:, gb + 1:gb + 16 * R + 1]))
+        i_d = V(v.tensor_tensor(T.dl[:, gb:gb + w], T.nen[:, 0:64].indirect(off), T.g2[:, gb + 1:gb + w + 1], A.add))
+        need("v", "vec", i_n)
+        i_e = V(v.tensor_copy(T.en0[:, eb:eb + R], T.s1[:, gb + 15:gb + w:16]))
+        need("v", "vec", max(i_d, i_e))
+        need("v", "act", max(i_vv[bt], i_fr))
+        i_s = V(v.tensor_copy(T.vv[:, vb:vb + WB * R].indirect(T.en0[:, eb:eb + R]), T.dl[:, gb:gb + w]))
+        return i_n, i_s, fill and fill()
 
-    def offsets(bt, bs, i_s):
-        out = []
+    def offsets(bt, bs, i_s, fill=None):
         need("v", "vec", i_s)
-        i1, i2 = [], []
+        i1 = []
         for b in bs:
-            p, c = 128 * (PB[bt] + b), VB[bt] + 128 * b
-            i1.append(V(v.tensor_tensor_scan(T.la[:, p:p + 128], T.d0[:, c:c + 128], T.vv[:, c:c + 128],
-                                             T.g2[:, GB[bt] + 16 * b:GB[bt] + 16 * b + 1], A.add, A.max)))
+            p, c = 128 * (PB[bt] + b), VB[bt] + WB * b
+            i1.append(V(v.tensor_tensor_scan(T.la[:, p:p + 128], T.fr[:], T.vv[:, c:c + 128],
+                                             T.g2[:, GB[bt] + 16 * b:GB[bt] + 16 * b + 1], A.add, A.add)))
         for b, i in zip(bs, i1):
             p = 128 * (PB[bt] + b)
             need("v", "vec", i)
-            i2.append(V(v.tensor_tensor_scan(T.lb[:, p:p + 128], T.dmk[:], T.la[:, p:p + 128], 0.0, A.add, A.max)))
-        for b, i in zip(bs, i2):
-            t = PB[bt] + b
-            need("v", "vec", i)
-            out.append(V(v.tensor_scalar(T.off[:, 32 * t:32 * t + 32], T.lb[:, 128 * t + 3:128 * t + 128:4],
-                                         T.cst[:], None, A.add)))
-        return out
+            i2 = V(v.tensor_tensor_scan(T.lb[:, p:p + 128], T.dmk[:], T.la[:, p:p + 128], 0.0, A.add, A.max))
+        t, n = PB[bt] + bs[0], len(bs)
+        x = fill and fill()
+        need("v", "vec", i2)
+        return V(v.tensor_scalar(T.off[:, 32 * t:32 * (t + n)], T.lb[:, 128 * t + 3:128 * (t + n):4], T.cst[:], None, A.add)), x
 
     def win(t):
         return T.xs[:, :].indirect(T.off[:, 32 * t:32 * t + 32])
@@ -289,105 +314,131 @@ def rank_program(g, core, T, topo):
         return T.qp[:, 128 * t:128 * t + 128]
 
     n_same = sum(len(lane_same(topo, T.cores[own[j]], core, at(own[j]))) for j in range(1, 4))
-    n_hand = 4 * (len(topo.engines(hs[0], T.cores[oth[0]])) // 2)
-
-    i_e, st = ends("M", 1, T.cdm[:, 0:1], False)
-    i7 = gather_s(7, offsets("M", [0], scatter("M", 1, i_e, st))[0])
+    n_list = 4 * (len(topo.engines(hs[0], T.cores[oth[0]])) // 2)
+    n_ends = 4 * len(topo.engines(hs[0], T.cores[oth[0]]))
 
     need("v", "cds", n_same)
-    i_e, st = ends("S", 3, T.cds[:, 0:3], False)
-    need("g", "vec", i_e)
-    fused([(T.cores[own[j]], T.el[:, 2 * (at(own[j]) - 1):2 * at(own[j]) - 1], T.en0[:, j - 1:j], "ens",
+    need("s", "cds", n_same)
+    i_n, i_s, _ = ends("S", 3, T.cds[:, 0:3], True)
+    need("g", "vec", i_n)
+    fused([(T.cores[own[j]], T.el[:, at(own[j]) - 1:at(own[j])], T.s1[:, 16 * j - 1:16 * j], "ens",
             lane_same(topo, core, T.cores[own[j]], j)) for j in range(1, 4)])
-    i_s = scatter("S", 3, i_e, st)
     i0 = gather_s(0, offsets("S", [0], i_s)[0])
-    o = offsets("S", [1, 2], i_s)
-    i2 = gather_s(2, o[1])
-    i1 = gather_v(1, o[0])
+    o, _ = offsets("S", [1, 2], i_s)
+    i1 = gather_s(1, o)
+    i2 = gather_s(2, o)
     quant(0, "act", i0)
-    quant(1, "vec", i1)
-    i = quant(2, "act", i2)
-    need("g", "vec", i)
-    to = [(T.cores[own[j]], at(own[j]) - 1, j) for j in range(1, 4)]
-    fused([(dc, u8(T.lc[:, 128 * s:128 * s + 128]), codes(j - 1), "t%d" % s, tile_same(topo, core, dc, j)) for dc, s, j in to])
-    fused([(dc, T.lp[:, 128 * s:128 * s + 128], plane(j - 1), "t%d" % s, tile_same(topo, core, dc, j)) for dc, s, j in to])
 
-    need("v", "cdo", n_hand)
-    need("s", "cdo", n_hand)
-    i_e, st = ends("O", 4, T.cdo[:, 0:4], True)
-    need("g", "vec", i_e)
-    fused([(hs[k], T.hen[:, 0:1], T.en0[:, 4 + k:5 + k], "hen", lane_up(topo, core, hs[k], k)) for k in range(4)])
-    i_s = scatter("O", 4, i_e, st)
+    need("v", "cdo", n_list)
+    i_n, i_s, i_q = ends("O", 4, T.cdo[:, 0:4], False, lambda: quant(1, "act", i1))
+    need("g", "vec", i_n)
+    fused([(hs[k], T.hen[:, 0:1], T.s1[:, GB["O"] + 16 * k + 15:GB["O"] + 16 * k + 16], "hen", ends_up(topo, core, hs[k], k))
+           for k in range(4)])
     i3 = gather_s(3, offsets("O", [0], i_s)[0])
-    i4 = gather_s(4, offsets("O", [1], i_s)[0])
-    o = offsets("O", [2, 3], i_s)
-    i5 = gather_s(5, o[0])
-    quant(3, "act", i3)
+
+    def across(js, what, eng, put):
+        fused([(T.cores[own[j]], put(at(own[j]) - 1), what(j - 1), "t%d" % (at(own[j]) - 1),
+                eng(topo, core, T.cores[own[j]], j)) for j in js])
+
+    need("g", "vec", i_q)
+    across((1, 2), codes, codes_same, lambda s: u8(T.lc[:, 128 * s:128 * s + 128]))
+    o, i_q = offsets("O", [1, 2], i_s, lambda: quant(2, "act", i2))
+    i4 = gather_s(4, o)
+    i5 = gather_s(5, o)
+    need("g", "vec", i_q)
+    across((3,), codes, codes_same, lambda s: u8(T.lc[:, 128 * s:128 * s + 128]))
+    across((1, 2, 3), plane, plane_same, lambda s: T.lp[:, 128 * s:128 * s + 128])
+
+    def up(ks, via, put, sem):
+        fused([(hs[k], u8(T.hc[:, 0:128]), codes(3 + k), "hc", codes_up(topo, core, hs[k], k)) for k in ks])
+        fused([(hs[h], put, plane(3 + k), sem, plane_up(topo, core, hs[h], k)) for k, h in zip(ks, via)])
+
+    o, _ = offsets("O", [3], i_s, lambda: quant(3, "act", i3))
     i = quant(4, "act", i4)
     need("g", "vec", i)
-    fused([(hs[k], u8(T.hc[:, 0:128]), codes(3 + k), "hc", codes_up(topo, core, hs[k], k)) for k in (0, 1)])
-    i6 = gather_v(6, o[1])
+    up((0, 1), (0, 1), T.hp[:, 0:128], "hp")
+    i6 = gather_v(6, o)
     quant(5, "act", i5)
     i = quant(6, "vec", i6)
     need("g", "vec", i)
-    fused([(hs[k], u8(T.hc[:, 0:128]), codes(3 + k), "hc", codes_up(topo, core, hs[k], k)) for k in (2, 3)])
-    fused([(hs[k], T.hp[:, 0:128], plane(3 + k), "hp", part(topo.engines(core, hs[k]), k, 4)) for k in range(4)])
+    up((3, 2), (0, 1), T.hp[:, 128:256], "hq")
 
-    i_own = quant(7, "act", i7)
     need("v", "lw", 16)
     i_w = V(v.quantize_mx(T.wc[:], T.wp[:], T.ws[:]))
-    V(v.tensor_scalar(T.en[:, 14:15], T.s1[:, GB["M"] + 15:GB["M"] + 16], -1.0, None, A.add))
+    i_l = V(v.tensor_copy(T.cdm[:, 0:1], T.cdu[:, rank:rank + 1]))
+    need("v", "vec", i_l)
+    need("s", "vec", i_l)
+    _, i_s, _ = ends("M", 1, T.cdm[:, 0:1], True)
 
-    def last(lo, n, sem, val):
-        need("v", sem, val)
-        i = V(v.tensor_scalar(T.ea[:, lo:lo + n], T.el[:, 2 * lo:2 * (lo + n) - 1:2], -1.0, None, A.add))
-        need("v", "vec", i)
-        i = V(v.tensor_scalar(T.eb[:, lo:lo + n], T.ea[:, lo:lo + n], 127, None, A.bitwise_and))
-        need("v", "vec", i)
-        return V(v.tensor_copy(T.en[:, 2 * lo:2 * (lo + n) - 1:2], T.eb[:, lo:lo + n]))
+    order = [2, 1, 0, 7, 3, 6, 4, 5]
+    first = {2: 0, 1: 0, 0: 0, 7: 3, 3: 4, 6: 4, 4: 4, 5: 4}
+    col = [0, 1, 2, 4, 6, 7, 8, 9]
 
-    def border(s):
-        return V(v.tensor_copy(T.mk[:, 136 * s + 8:136 * s + 136].indirect(T.en[:, 2 * s:2 * s + 1]), T.neg[:]))
+    def places(slots, sem, val):
+        need("s", sem, val)
+        for s in slots:
+            p = order.index(s)
+            b = (-(s + 1)) % 4 - 1 if s < 3 else (3 - s) % 4
+            i = S(sc.activation(T.ef[:, col[p]:col[p] + 1], T.el[:, s:s + 1], F.Copy,
+                                bias=float(128 * (p - first[s]) - WB * b - 1)))
+        return i
 
-    i = last(0, 3, "ens", n_same)
-    need("v", "vec", i)
+    def last(slots, i):
+        c = col[order.index(slots[0])]
+        need("v", "act", i)
+        return V(v.tensor_copy(T.en[:, c:c + len(slots)], T.ef[:, c:c + len(slots)]))
+
+    def border(slots):
+        p, n = order.index(slots[0]), len(slots)
+        return V(v.tensor_copy(T.mk[:, 128 * p + 8:128 * (p + n) + 8].indirect(T.en[:, col[p]:col[p] + n]), T.neg[:, 0:16 * n]))
+
+    i_f = places((2, 1, 0), "ens", n_same)
+    i7 = gather_s(7, offsets("M", [0], i_s)[0])
+    i_g = places((3, 6, 4, 5), "eno", n_ends)
+    V(v.tensor_scalar(T.en[:, 4:5], T.s1[:, GB["M"] + 15:GB["M"] + 16], -1.0, None, A.add))
+    i = last((2, 1, 0), i_f)
     need("v", "act", i_mk)
-    brd = {s: border(s) for s in (7, 2, 1, 0)}
+    need("v", "vec", i)
+    i_b = [border((2, 1, 0)), border((7,))]
 
     def tile_engines(s):
         if s >= 3:
             return 2 * len(topo.engines(hs[0], T.cores[oth[0]]))
         j = (-(s + 1)) % 4
-        return 2 * len(tile_same(topo, T.cores[own[s + 1]], core, j))
+        return sum(len(f(topo, T.cores[own[s + 1]], core, j)) for f in (codes_same, plane_same))
 
-    def score(s):
-        ps = T.ps[:, 512 * s:512 * s + 128]
-        need("t", "vec", i_w)
-        if s == 7:
-            need("t", "vec", i_own)
-            i = done("pe", pe.matmul_mx(ps, T.wc[:], T.wp[:], T.qc[:, 896:1024], T.qp[:, 896:1024], True, True))
-            q = rank
-        else:
-            need("t", "t%d" % s, tile_engines(s))
-            i = done("pe", pe.matmul_mx(ps, T.wc[:], T.wp[:], T.lc[:, 128 * s:128 * s + 128],
-                                        T.lp[:, 128 * s:128 * s + 128], True, True))
-            q = own[s + 1] if s < 3 else oth[s - 3]
-        need("v", "pe", i)
-        need("v", "vec", brd[s])
-        i = V(v.tensor_tensor_scan(T.so[:, 128 * s:128 * s + 128], T.mk[:, 136 * s + 7:136 * s + 135], ps, -BIG, A.min, A.max))
+    def score(slots):
+        for s in slots:
+            p = order.index(s)
+            ps = T.ps[:, 512 * s:512 * s + 128]
+            need("t", "vec", i_w)
+            if s == 7:
+                need("t", "vec", i_own)
+                i = done("pe", pe.matmul_mx(ps, T.wc[:], T.wp[:], T.qc[:, 896:1024], T.qp[:, 896:1024], True, True))
+            else:
+                need("t", "t%d" % s, tile_engines(s))
+                i = done("pe", pe.matmul_mx(ps, T.wc[:], T.wp[:], T.lc[:, 128 * s:128 * s + 128],
+                                            T.lp[:, 128 * s:128 * s + 128], True, True))
+            need("v", "pe", i)
+            need("v", "vec", i_b[-1])
+            i = V(v.tensor_tensor_scan(T.so[:, 128 * p:128 * p + 128], T.mk[:, 128 * p + 7:128 * p + 135], ps, -BIG, A.min, A.max))
         need("s", "vec", i)
-        i = S(sc.activation(T.ys[:, 16 * q:16 * q + 16], T.so[:, 128 * s:128 * s + 128].indirect(T.en[:, 2 * s:2 * s + 1]), F.Copy))
+        p, n, f = order.index(slots[0]), len(slots), first[slots[0]]
+        i = S(sc.activation(T.ys[:, 16 * p:16 * (p + n)], T.so[:, 128 * f:128 * (p + n)].indirect(T.en[:, col[p]:col[p] + n]), F.Copy))
         need("y", "act", i)
-        g.sync.dma_start(T.y[:, 16 * q:16 * q + 16], T.ys[:, 16 * q:16 * q + 16]).then_inc(T.sem.ly, 16)
+        for s in slots:
+            p = order.index(s)
+            q = rank if s == 7 else own[s + 1] if s < 3 else oth[s - 3]
+            g.sync.dma_start(T.y[:, 16 * q:16 * q + 16], T.ys[:, 16 * p:16 * p + 16]).then_inc(T.sem.ly, 16)
 
-    for s in (7, 2, 1, 0):
-        score(s)
-    i = last(3, 4, "eno", n_hand)
+    score((2, 1, 0))
+    i_own = quant(7, "act", i7)
+    score((7,))
+    i = last((3, 6, 4, 5), i_g)
     need("v", "vec", i)
-    for s in (3, 6, 5, 4):
-        brd[s] = border(s)
-    for s in (3, 6, 5, 4):
-        score(s)
+    i_b.append(border((3, 6, 4, 5)))
+    score((3, 6))
+    score((4, 5))
 
     for sem in ("vec", "act", "pe", "gc", "sent"):
         need("g", sem, cnt[sem])

from concourse.bass import DstId, RemoteDMATransfer
from concourse.mybir import dt, AluOpType as A, ActivationFunctionType as F

N, TOK, CAP = 8, 512, 128
BIG, FAR, LIFT = 1.0e29, 1.0e6, 4096.0
WB = 136
VB = {"S": 0, "O": 408, "M": 952}
GB = {"S": 0, "O": 56, "M": 128}
EB = {"S": 0, "O": 4, "M": 8}
PB = {"S": 0, "O": 3, "M": 7}
CARRY = {0: (0, 3), 1: (1, 2)}

SCRATCH = {
    "cdi": ("sbuf", [128, 8], "int32"), "cdu": ("sbuf", [128, 8], "uint16"), "cdm": ("sbuf", [128, 2], "uint16"),
    "row": ("sbuf", [1, 128], "int32"), "tab": ("sbuf", [128, 128], "int32"),
    "stt": ("sbuf", [128, 64], "float32"), "lnt": ("sbuf", [128, 64], "float32"),
    "nes": ("sbuf", [128, 64], "float32"), "nen": ("sbuf", [128, 64], "float32"),
    "poi": ("sbuf", [128, 4], "int32"), "poa": ("sbuf", [128, 4], "int32"), "pou": ("sbuf", [128, 4], "uint16"),
    "pp": ("sbuf", [128, 1], "int32"), "ki": ("sbuf", [128, 3], "int32"), "kf": ("sbuf", [128, 3], "float32"),
    "csu": ("sbuf", [128, 1], "float32"), "cst": ("sbuf", [128, 1], "float32"), "zz": ("sbuf", [128, 1032], "bfloat16"),
    "ii": ("sbuf", [128, 64], "float32"), "jj": ("sbuf", [128, 128], "float32"),
    "le": ("sbuf", [128, 64], "float32"), "dmb": ("sbuf", [128, 128], "float32"), "dmk": ("sbuf", [128, 128], "float32"),
    "rst": ("sbuf", [128, 64], "float32"), "fr": ("sbuf", [128, 128], "float32"), "neg": ("sbuf", [128, 64], "float32"),
    "cds": ("sbuf", [128, 4], "uint16"), "cdo": ("sbuf", [128, 4], "uint16"),
    "g1": ("sbuf", [128, 152], "float32"), "s1": ("sbuf", [128, 152], "float32"), "g2": ("sbuf", [128, 152], "float32"),
    "dl": ("sbuf", [128, 152], "float32"), "en0": ("sbuf", [128, 16], "uint16"),
    "vv": ("sbuf", [128, 1088], "float32"),
    "la": ("sbuf", [128, 1024], "float32"), "lb": ("sbuf", [128, 1024], "float32"),
    "off": ("sbuf", [128, 256], "uint16"),
    "xs": ("sbuf", [128, 4 * (TOK + CAP)], "bfloat16"), "ws": ("sbuf", [128, 512], "bfloat16"),
    "tile": ("sbuf", [128, 4096], "bfloat16"),
    "qc": ("sbuf", [128, 1024], "float8_e4m3fn_x4"), "qp": ("sbuf", [128, 1024], "uint8"),
    "wc": ("sbuf", [128, 128], "float8_e4m3fn_x4"), "wp": ("sbuf", [128, 128], "uint8"),
    "lc": ("sbuf", [128, 896], "float8_e4m3fn_x4"), "lp": ("sbuf", [128, 896], "uint8"),
    "el": ("sbuf", [128, 8], "float32"), "ef": ("sbuf", [128, 12], "float32"), "en": ("sbuf", [128, 12], "uint16"),
    "mk": ("sbuf", [128, 1032], "float32"), "so": ("sbuf", [128, 1024], "float32"), "ys": ("sbuf", [128, 128], "float32"),
    "ps": ("psum", [128, 4096], "float32"),
    "hcd": ("sbuf", [128, 8], "uint16"), "hen": ("sbuf", [128, 1], "float32"),
    "hc": ("sbuf", [128, 128], "float8_e4m3fn_x4"), "hp": ("sbuf", [128, 256], "uint8"),
}
SEMAPHORES = (["vec", "act", "pe", "gc", "lcd", "ltab", "lx", "lw", "ly", "sent", "cds", "cdo", "ens", "eno",
               "hcd", "hen", "hc", "hp", "hq"] + ["t%d" % s for s in range(7)])


def groups(T, topo, r):
    own = [q for q in range(N) if q == r or topo.may_write(T.cores[r], T.cores[q])]
    oth = [q for q in range(N) if q not in own]
    a = own.index(r)
    return [own[(a + j) % len(own)] for j in range(len(own))], [oth[(a + k) % len(oth)] for k in range(len(oth))], a


def helpers(T, topo, r):
    c = T.cores[r]
    dst = T.cores[groups(T, topo, r)[1][0]]
    hs = [h for h in topo.cores_of(c) if h != c and topo.may_write(h, dst)]
    near = [h for h in hs if topo.die(h) == topo.die(c)]
    far = [h for h in hs if topo.die(h) != topo.die(c)]
    return [near[0], far[0], near[1], far[1]]


def part(e, i, n):
    w = len(e) // n
    return e[i * w:(i + 1) * w]


def bits(e):
    return sum(1 << x for x in e)


def upper(topo, c, h):
    e = topo.engines(c, h)
    return e[len(e) // 2:]


def lists_up(topo, c, h, k):
    return part(upper(topo, c, h), k, 2)


def ends_up(topo, c, h, k):
    return part(upper(topo, c, h), k, 4)


def codes_up(topo, c, h, k):
    return part(upper(topo, c, h), k, 2) if k in CARRY else part(topo.engines(c, h), k - 2, 2)


def plane_up(topo, c, h, k):
    return part(topo.engines(c, h), k, 4) if k in CARRY else part(topo.engines(c, h), k - 2, 2)


def lane_same(topo, c, d, j):
    return part(topo.engines(c, d), j - 1, 4)


def codes_same(topo, c, d, j):
    e = topo.engines(c, d)
    return part(e, j - 1, 2) if j < 3 else e


def plane_same(topo, c, d, j):
    e = topo.engines(c, d)
    return part(e, j - 1, 4) if j < 3 else part(e, 1, 2)


def u8(ap):
    return ap.bitcast(dt.uint8)


def hand_on(g, core, T, topo, r, k):
    _, oth, a = groups(T, topo, r)
    rc = T.cores[r]
    sent = [0]

    def slot(n):
        return (a - groups(T, topo, oth[n])[2]) % 4

    def to(n):
        return T.cores[oth[n]]

    def on(n, dst, src, sem, eng):
        rid, pid = topo.addr(to(n), core)
        g.remote_dma(dst, src, T.sem[sem], T.sem.sent, pid, rid, bits(eng))
        sent[0] += len(eng)

    if k in CARRY:
        g.wait_ge(T.sem.hcd, len(lists_up(topo, rc, core, k)))
        ts = []
        for i, n in enumerate(CARRY[k]):
            rid, pid = topo.addr(to(n), core)
            e = part(topo.engines(core, to(n)), i, 2)
            ts.append(RemoteDMATransfer(dst_ids=[DstId(rid=rid, pnc=pid)], dma_engine_mask=bits(e), remote_sem=T.sem.cdo,
                                        src=T.hcd[:, oth[n]:oth[n] + 1], dst=T.cdo[:, slot(n):slot(n) + 1]))
            sent[0] += len(e)
        g.remote_dma_fused(ts, local_sem=T.sem.sent)
    e = topo.engines(core, to(k))
    g.wait_ge(T.sem.hen, len(ends_up(topo, rc, core, k)))
    on(k, T.el[:, 3 + slot(k):4 + slot(k)], T.hen[:, 0:1], "eno", e)
    s = 3 + slot(k)
    g.wait_ge(T.sem.hc, len(codes_up(topo, rc, core, k)))
    on(k, u8(T.lc[:, 128 * s:128 * s + 128]), u8(T.hc[:, 0:128]), "t%d" % s, e)
    if k in CARRY:
        for i, n in enumerate(CARRY[k]):
            s = 3 + slot(n)
            g.wait_ge(T.sem["hp" if i == 0 else "hq"], len(plane_up(topo, rc, core, n)))
            on(n, T.lp[:, 128 * s:128 * s + 128], T.hp[:, 128 * i:128 * i + 128], "t%d" % s, topo.engines(core, to(n)))
    g.wait_ge(T.sem.sent, sent[0])


def rank_program(g, core, T, topo):
    rank = T.rank_of(core)
    if rank is None:
        for r in range(N):
            if T.cores[r] in topo.cores_of(core):
                hs = helpers(T, topo, r)
                if core in hs:
                    hand_on(g, core, T, topo, r, hs.index(core))
        return
    own, oth, a = groups(T, topo, rank)
    hs = helpers(T, topo, rank)
    v, sc, pe = g.vector, g.scalar, g.tensor
    queue = {"v": v, "s": sc, "t": pe, "g": g, "y": g.sync}
    cnt = {"vec": 0, "act": 0, "pe": 0, "gc": 0, "sent": 0}
    seen = {}

    def need(q, sem, val):
        if seen.get((q, sem), 0) < val:
            queue[q].wait_ge(T.sem[sem], int(val))
            seen[(q, sem)] = val

    def done(sem, ins):
        cnt[sem] += 1
        ins.then_inc(T.sem[sem], 1)
        return cnt[sem]

    def V(ins):
        return done("vec", ins)

    def S(ins):
        return done("act", ins)

    for i in range(8):
        (g.sync if i % 2 == 0 else sc).dma_start(T.cdi[16 * i:16 * i + 16, :], T.cd[:]).then_inc(T.sem.lcd, 16)
    g.sync.dma_start(T.row[0:1, 0:64], T.st[:]).then_inc(T.sem.ltab, 16)
    sc.dma_start(T.row[0:1, 64:128], T.ln[:]).then_inc(T.sem.ltab, 16)
    g.sync.dma_start(T.xs[:, 0:4 * TOK], T.x[:]).then_inc(T.sem.lx, 16)
    sc.dma_start(T.ws[:], T.qw[:]).then_inc(T.sem.lw, 16)

    done("gc", g.iota(T.pp[:], [[0, 1]], 0, 1))
    i_io = done("gc", g.iota(T.poi[:], [[1, 4]], 0, 4))
    done("gc", g.iota(T.ii[:], [[0, 4], [1, 16]], 0, 0, allow_small_or_imprecise_dtypes=True))
    done("gc", g.iota(T.jj[:], [[0, 32], [1, 4]], 0, 0, allow_small_or_imprecise_dtypes=True))

    i_z = V(v.memset(T.zz[:], 0.0))
    need("s", "vec", i_z)
    i_vv = {}
    for bt, R in (("S", 3), ("O", 4), ("M", 1)):
        i_vv[bt] = S(sc.activation(T.vv[:, VB[bt]:VB[bt] + WB * R], T.zz[:, 0:WB * R], F.Copy))
    i_fr = S(sc.activation(T.fr[:], T.zz[:, 0:128], F.Copy, bias=4.0))
    S(sc.activation(T.neg[:], T.zz[:, 0:64], F.Copy, bias=-BIG))
    i_mk = S(sc.activation(T.mk[:], T.zz[:], F.Copy, bias=BIG))
    need("v", "gc", i_io)
    V(v.tensor_scalar(T.ki[:, 0:1], T.pp[:], 15, None, A.bitwise_and))
    V(v.tensor_scalar(T.ki[:, 1:2], T.pp[:], 3, None, A.bitwise_and))
    V(v.tensor_scalar(T.ki[:, 2:3], T.pp[:], 15, 2, A.bitwise_and, A.arith_shift_right))
    i_p = V(v.tensor_scalar(T.poa[:], T.poi[:], 63, None, A.bitwise_and))

    need("v", "lcd", 128)
    i_cd = V(v.tensor_copy(T.cdu[:], T.cdi[:]))
    need("g", "vec", i_cd)

    def fused(trs):
        ts = []
        for dc, dst, src, sem, e in trs:
            rid, pid = topo.addr(dc, core)
            ts.append(RemoteDMATransfer(dst_ids=[DstId(rid=rid, pnc=pid)], dma_engine_mask=bits(e),
                                        remote_sem=T.sem[sem], src=src, dst=dst))
            cnt["sent"] += len(e)
        g.remote_dma_fused(ts, local_sem=T.sem.sent)

    def at(d):
        return (a - groups(T, topo, d)[2]) % 4

    fused([(T.cores[own[j]], T.cds[:, at(own[j]) - 1:at(own[j])], T.cdu[:, own[j]:own[j] + 1], "cds",
            lane_same(topo, core, T.cores[own[j]], j)) for j in range(1, 4)])
    fused([(hs[k], T.hcd[:, 0:8], T.cdu[:, 0:8], "hcd", lists_up(topo, core, hs[k], k)) for k in CARRY])
    need("g", "ltab", 32)
    i_tab = done("gc", g.partition_broadcast(T.tab[:], T.row[0:1, :], 128))

    need("v", "vec", i_p)
    V(v.tensor_copy(T.kf[:], T.ki[:]))
    i_k = V(v.tensor_copy(T.pou[:], T.poa[:]))
    i_r = V(v.memset(T.rst[:], 0.0))
    need("v", "gc", 4)
    need("v", "vec", i_k)
    V(v.tensor_scalar(T.le[:], T.ii[:], T.kf[:, 0:1], None, A.is_le))
    i_m = V(v.tensor_scalar(T.dmb[:], T.jj[:], T.kf[:, 2:3], FAR + LIFT, A.is_gt, A.mult))
    i_c = V(v.tensor_scalar(T.csu[:], T.kf[:, 2:3], -3.0, LIFT, A.add, A.mult))
    need("v", "vec", i_r)
    for b in range(1, 4):
        V(v.memset(T.rst[:, 16 * b:16 * b + 1], float(WB * b)))
    need("v", "vec", i_m)
    V(v.tensor_scalar(T.dmk[:], T.dmb[:], -FAR, None, A.add))
    need("v", "vec", i_c)
    V(v.tensor_scalar(T.cst[:], T.csu[:], T.kf[:, 1:2], -4.0, A.add, A.add))
    V(v.memset(T.g2[:], 0.0))
    V(v.memset(T.xs[:, 4 * TOK:], 0.0))
    need("v", "gc", i_tab)
    i_ln = V(v.tensor_copy(T.lnt[:], T.tab[:, 64:128].indirect(T.pou[:, 0:4])))
    i_st = V(v.tensor_scalar(T.stt[:], T.tab[:, 0:64].indirect(T.pou[:, 0:4]), 4.0, None, A.mult))
    need("v", "vec", i_ln)
    i = V(v.tensor_scalar(T.nes[:], T.lnt[:], -4.0, None, A.mult))
    need("v", "vec", i)
    i_ne = V(v.tensor_tensor(T.nen[:], T.nes[:], T.stt[:], A.subtract))

    def ends(bt, R, off, on_s, fill=None):
        gb, eb, vb = GB[bt], EB[bt], VB[bt]
        w = 16 * R
        need("v", "vec", i_ne)
        if on_s:
            need("s", "vec", i_st)
            st = ("act", S(sc.activation(T.g2[:, gb:gb + w], T.stt[:, 0:64].indirect(off), F.Copy)))
        i = V(v.tensor_tensor(T.g1[:, gb:gb + w], T.lnt[:, 0:64].indirect(off), T.le[:, 0:w], A.mult))
        if not on_s:
            st = ("vec", V(v.tensor_copy(T.g2[:, gb:gb + w], T.stt[:, 0:64].indirect(off))))
        need("v", "vec", i)
        i_n = V(v.tensor_tensor_scan(T.s1[:, gb:gb + w], T.rst[:, 0:w], T.g1[:, gb:gb + w], 0.0, A.max, A.add))
        need("v", *st)
        i_d = V(v.tensor_tensor(T.dl[:, gb:gb + w], T.nen[:, 0:64].indirect(off), T.g2[:, gb + 1:gb + w + 1], A.add))
        need("v", "vec", i_n)
        i_e = V(v.tensor_copy(T.en0[:, eb:eb + R], T.s1[:, gb + 15:gb + w:16]))
        need("v", "vec", max(i_d, i_e))
        need("v", "act", max(i_vv[bt], i_fr))
        i_s = V(v.tensor_copy(T.vv[:, vb:vb + WB * R].indirect(T.en0[:, eb:eb + R]), T.dl[:, gb:gb + w]))
        return i_n, i_s, fill and fill()

    def offsets(bt, bs, i_s, fill=None):
        need("v", "vec", i_s)
        i1 = []
        for b in bs:
            p, c = 128 * (PB[bt] + b), VB[bt] + WB * b
            i1.append(V(v.tensor_tensor_scan(T.la[:, p:p + 128], T.fr[:], T.vv[:, c:c + 128],
                                             T.g2[:, GB[bt] + 16 * b:GB[bt] + 16 * b + 1], A.add, A.add)))
        for b, i in zip(bs, i1):
            p = 128 * (PB[bt] + b)
            need("v", "vec", i)
            i2 = V(v.tensor_tensor_scan(T.lb[:, p:p + 128], T.dmk[:], T.la[:, p:p + 128], 0.0, A.add, A.max))
        t, n = PB[bt] + bs[0], len(bs)
        x = fill and fill()
        need("v", "vec", i2)
        return V(v.tensor_scalar(T.off[:, 32 * t:32 * (t + n)], T.lb[:, 128 * t + 3:128 * (t + n):4], T.cst[:], None, A.add)), x

    def win(t):
        return T.xs[:, :].indirect(T.off[:, 32 * t:32 * t + 32])

    def gather_s(t, i):
        need("s", "lx", 16)
        need("s", "vec", i)
        return S(sc.activation(T.tile[:, 512 * t:512 * t + 512], win(t), F.Copy))

    def gather_v(t, i):
        need("v", "lx", 16)
        need("v", "vec", i)
        return V(v.tensor_copy(T.tile[:, 512 * t:512 * t + 512], win(t)))

    def quant(t, sem, i):
        need("v", sem, i)
        return V(v.quantize_mx(T.qc[:, 128 * t:128 * t + 128], T.qp[:, 128 * t:128 * t + 128],
                               T.tile[:, 512 * t:512 * t + 512]))

    def codes(t):
        return u8(T.qc[:, 128 * t:128 * t + 128])

    def plane(t):
        return T.qp[:, 128 * t:128 * t + 128]

    n_same = sum(len(lane_same(topo, T.cores[own[j]], core, at(own[j]))) for j in range(1, 4))
    n_list = 4 * (len(topo.engines(hs[0], T.cores[oth[0]])) // 2)
    n_ends = 4 * len(topo.engines(hs[0], T.cores[oth[0]]))

    need("v", "cds", n_same)
    need("s", "cds", n_same)
    i_n, i_s, _ = ends("S", 3, T.cds[:, 0:3], True)
    need("g", "vec", i_n)
    fused([(T.cores[own[j]], T.el[:, at(own[j]) - 1:at(own[j])], T.s1[:, 16 * j - 1:16 * j], "ens",
            lane_same(topo, core, T.cores[own[j]], j)) for j in range(1, 4)])
    i0 = gather_s(0, offsets("S", [0], i_s)[0])
    o, _ = offsets("S", [1, 2], i_s)
    i1 = gather_s(1, o)
    i2 = gather_s(2, o)
    quant(0, "act", i0)

    need("v", "cdo", n_list)
    i_n, i_s, i_q = ends("O", 4, T.cdo[:, 0:4], False, lambda: quant(1, "act", i1))
    need("g", "vec", i_n)
    fused([(hs[k], T.hen[:, 0:1], T.s1[:, GB["O"] + 16 * k + 15:GB["O"] + 16 * k + 16], "hen", ends_up(topo, core, hs[k], k))
           for k in range(4)])
    i3 = gather_s(3, offsets("O", [0], i_s)[0])

    def across(js, what, eng, put):
        fused([(T.cores[own[j]], put(at(own[j]) - 1), what(j - 1), "t%d" % (at(own[j]) - 1),
                eng(topo, core, T.cores[own[j]], j)) for j in js])

    need("g", "vec", i_q)
    across((1, 2), codes, codes_same, lambda s: u8(T.lc[:, 128 * s:128 * s + 128]))
    o, i_q = offsets("O", [1, 2], i_s, lambda: quant(2, "act", i2))
    i4 = gather_s(4, o)
    i5 = gather_s(5, o)
    need("g", "vec", i_q)
    across((3,), codes, codes_same, lambda s: u8(T.lc[:, 128 * s:128 * s + 128]))
    across((1, 2, 3), plane, plane_same, lambda s: T.lp[:, 128 * s:128 * s + 128])

    def up(ks, via, put, sem):
        fused([(hs[k], u8(T.hc[:, 0:128]), codes(3 + k), "hc", codes_up(topo, core, hs[k], k)) for k in ks])
        fused([(hs[h], put, plane(3 + k), sem, plane_up(topo, core, hs[h], k)) for k, h in zip(ks, via)])

    o, _ = offsets("O", [3], i_s, lambda: quant(3, "act", i3))
    i = quant(4, "act", i4)
    need("g", "vec", i)
    up((0, 1), (0, 1), T.hp[:, 0:128], "hp")
    i6 = gather_v(6, o)
    quant(5, "act", i5)
    i = quant(6, "vec", i6)
    need("g", "vec", i)
    up((3, 2), (0, 1), T.hp[:, 128:256], "hq")

    need("v", "lw", 16)
    i_w = V(v.quantize_mx(T.wc[:], T.wp[:], T.ws[:]))
    i_l = V(v.tensor_copy(T.cdm[:, 0:1], T.cdu[:, rank:rank + 1]))
    need("v", "vec", i_l)
    need("s", "vec", i_l)
    _, i_s, _ = ends("M", 1, T.cdm[:, 0:1], True)

    order = [2, 1, 0, 7, 3, 6, 4, 5]
    first = {2: 0, 1: 0, 0: 0, 7: 3, 3: 4, 6: 4, 4: 4, 5: 4}
    col = [0, 1, 2, 4, 6, 7, 8, 9]

    def places(slots, sem, val):
        need("s", sem, val)
        for s in slots:
            p = order.index(s)
            b = (-(s + 1)) % 4 - 1 if s < 3 else (3 - s) % 4
            i = S(sc.activation(T.ef[:, col[p]:col[p] + 1], T.el[:, s:s + 1], F.Copy,
                                bias=float(128 * (p - first[s]) - WB * b - 1)))
        return i

    def last(slots, i):
        c = col[order.index(slots[0])]
        need("v", "act", i)
        return V(v.tensor_copy(T.en[:, c:c + len(slots)], T.ef[:, c:c + len(slots)]))

    def border(slots):
        p, n = order.index(slots[0]), len(slots)
        return V(v.tensor_copy(T.mk[:, 128 * p + 8:128 * (p + n) + 8].indirect(T.en[:, col[p]:col[p] + n]), T.neg[:, 0:16 * n]))

    i_f = places((2, 1, 0), "ens", n_same)
    i7 = gather_s(7, offsets("M", [0], i_s)[0])
    i_g = places((3, 6, 4, 5), "eno", n_ends)
    V(v.tensor_scalar(T.en[:, 4:5], T.s1[:, GB["M"] + 15:GB["M"] + 16], -1.0, None, A.add))
    i = last((2, 1, 0), i_f)
    need("v", "act", i_mk)
    need("v", "vec", i)
    i_b = [border((2, 1, 0)), border((7,))]

    def tile_engines(s):
        if s >= 3:
            return 2 * len(topo.engines(hs[0], T.cores[oth[0]]))
        j = (-(s + 1)) % 4
        return sum(len(f(topo, T.cores[own[s + 1]], core, j)) for f in (codes_same, plane_same))

    def score(slots):
        for s in slots:
            p = order.index(s)
            ps = T.ps[:, 512 * s:512 * s + 128]
            need("t", "vec", i_w)
            if s == 7:
                need("t", "vec", i_own)
                i = done("pe", pe.matmul_mx(ps, T.wc[:], T.wp[:], T.qc[:, 896:1024], T.qp[:, 896:1024], True, True))
            else:
                need("t", "t%d" % s, tile_engines(s))
                i = done("pe", pe.matmul_mx(ps, T.wc[:], T.wp[:], T.lc[:, 128 * s:128 * s + 128],
                                            T.lp[:, 128 * s:128 * s + 128], True, True))
            need("v", "pe", i)
            need("v", "vec", i_b[-1])
            i = V(v.tensor_tensor_scan(T.so[:, 128 * p:128 * p + 128], T.mk[:, 128 * p + 7:128 * p + 135], ps, -BIG, A.min, A.max))
        need("s", "vec", i)
        p, n, f = order.index(slots[0]), len(slots), first[slots[0]]
        i = S(sc.activation(T.ys[:, 16 * p:16 * (p + n)], T.so[:, 128 * f:128 * (p + n)].indirect(T.en[:, col[p]:col[p] + n]), F.Copy))
        need("y", "act", i)
        for s in slots:
            p = order.index(s)
            q = rank if s == 7 else own[s + 1] if s < 3 else oth[s - 3]
            g.sync.dma_start(T.y[:, 16 * q:16 * q + 16], T.ys[:, 16 * p:16 * p + 16]).then_inc(T.sem.ly, 16)

    score((2, 1, 0))
    i_own = quant(7, "act", i7)
    score((7,))
    i = last((3, 6, 4, 5), i_g)
    need("v", "vec", i)
    i_b.append(border((3, 6, 4, 5)))
    score((3, 6))
    score((4, 5))

    for sem in ("vec", "act", "pe", "gc", "sent"):
        need("g", sem, cnt[sem])
    need("g", "ly", 128)
